import numpy as np
import ml_dtypes


def mxq(x, axis, fmt="e4m3"):
    dtype, down = {"e4m3": (ml_dtypes.float8_e4m3fn, 7), "e5m2": (ml_dtypes.float8_e5m2, 14)}[fmt]
    v = np.moveaxis(np.asarray(x, np.float32).astype(ml_dtypes.bfloat16).astype(np.float64), axis, -1)
    blocks = v.reshape(v.shape[:-1] + (-1, 32))
    amax = np.abs(blocks).max(-1, keepdims=True)
    byte = np.maximum(np.where(amax > 0, np.frexp(amax)[1] - 1 + 127, 0) - down, 1)
    scale = np.exp2(byte - 127.0)
    codes = (blocks / scale).astype(np.float32).astype(dtype).astype(np.float64)
    return np.moveaxis((codes * scale).reshape(v.shape), -1, axis)


WIDE = False


def mx_kscale(k):
    if not WIDE:
        return np.ones(k)
    levels = np.array([10, -10, 5, -5, 0])
    if k % 512:
        return np.exp2(np.random.permutation(np.resize(levels, k // 32))).repeat(32)
    a = np.empty((k // 512, 16))
    for p in range(k // 512):
        a[p, :8] = np.random.permutation(np.resize(levels, 8))
        for g in range(8):
            far = levels[np.abs(levels - a[p, g]) >= 10]
            a[p, g + 8] = far[np.random.randint(len(far))]
    return np.exp2(a.ravel()).repeat(32)


def f64(x):
    return np.asarray(x).astype(np.float64)


def striped(idx):
    return np.tile(idx.reshape(-1, 16).T, (8, 1)).astype(np.uint16)


def unstriped(offs):
    return offs[:16].T.reshape(-1).astype(np.int64)

def planes(y):
    n, m = y.shape
    v = y.astype(np.float32).astype(ml_dtypes.bfloat16).astype(np.float64).reshape(n // 32, 32, m)
    top = np.abs(v).max(1)
    byte = np.clip(np.where(top > 0, np.frexp(top)[1] - 1 + 127 - 7, 1), 1, 254)
    codes = (v * np.exp2(127.0 - byte)[:, None, :]).reshape(n, m).astype(np.float32).astype(ml_dtypes.float8_e4m3fn).view(np.uint8)
    words = codes.reshape(n // 512, 128, 4, m).transpose(0, 1, 3, 2)
    return np.ascontiguousarray(words), np.ascontiguousarray(byte.astype(np.uint8).reshape(n // 512, 16, m))


K, T, S, N, U = 512, 2048, 512, 512, 1024


def setup_inputs():
    n = np.random.standard_normal
    s = mx_kscale(K)[:, None]
    return {
        "xT": (n((K, T)) * s).astype(np.float32),
        "w1": (n((K, N)) / np.sqrt(K) / s).astype(np.float32),
        "scale": np.random.uniform(0.5, 1.5, (N, U)).astype(np.float32),
        "offs": striped(np.random.permutation(T)[:S]),
        "task": striped(np.random.permutation(U)[(U * np.random.uniform(0, 1, S) ** 4).astype(np.int64)]),
    }


def reference(xT, w1, scale, offs, task):
    xq = mxq(f64(xT)[:, unstriped(offs)], 0, "e4m3")
    y = mxq(f64(w1), 0, "e4m3").T @ xq
    g = f64(scale)[:, unstriped(task)]
    out_0 = y * g
    return (out_0,) + planes(out_0)

@@ -1,0 +1,115 @@
+from contextlib import ExitStack
+
+import concourse.mybir as mybir
+
+K, T, S, N, U = 512, 2048, 512, 512, 1024
+FLOPS = 2 * K * N * S
+
+F32 = mybir.dt.float32
+BF16 = mybir.dt.bfloat16
+I32 = mybir.dt.int32
+U32 = mybir.dt.uint32
+U16 = mybir.dt.uint16
+U8 = mybir.dt.uint8
+FP8X4 = mybir.dt.float8_e4m3fn_x4
+MULT = mybir.AluOpType.mult
+
+P = 128
+PACK = 4
+HALF = S // 2
+
+
+def tile_picked_none_lo_kernel(tc, xT, w1, scale, offs, task, out_0, out_1, out_2):
+    nc = tc.nc
+    x_rows = xT.rearrange("(p j) c -> p j c", j=PACK)
+    w_rows = w1.rearrange("(p j) c -> p j c", j=PACK)
+    scale_rows = scale.rearrange("(p t) c -> p t c", t=PACK)
+    out_rows = out_0.rearrange("(p t) c -> p t c", t=PACK)
+    out_words = out_1[0].rearrange("p c r -> p (c r)").bitcast(I32)
+    out_scales = out_2[0].bitcast(I32)
+
+    with ExitStack() as ctx:
+        sb = ctx.enter_context(tc.tile_pool(name="sb", bufs=1))
+        psum = ctx.enter_context(tc.psum_pool(name="psum", bufs=1))
+
+        offs_sb = sb.tile([P, S // 16], U16, name="offs_sb")
+        task_sb = sb.tile([P, S // 16], U16, name="task_sb")
+        x_sb = [sb.tile([P, T], F32, name=f"x_sb{j}") for j in range(PACK)]
+        w_sb = [sb.tile([P, PACK, N // 2], F32, name=f"w_sb{h}") for h in range(2)]
+        scale_sb = [sb.tile([P, U], F32, name=f"scale_sb{t}") for t in range(PACK)]
+
+        nc.sync.dma_start(x_sb[0][:], x_rows[:, 0, :])
+        nc.sync.dma_start(offs_sb[:], offs)
+        for j in range(1, PACK):
+            nc.sync.dma_start(x_sb[j][:], x_rows[:, j, :])
+        for h in range(2):
+            nc.sync.dma_start(w_sb[h][:], w_rows[:, :, h * (N // 2) : (h + 1) * (N // 2)])
+        nc.sync.dma_start(task_sb[:], task)
+        for t in range(PACK):
+            nc.sync.dma_start(scale_sb[t][:], scale_rows[:, t, :])
+
+        x_bf = sb.tile([P, S, PACK], BF16, align_bytes=64, name="x_bf")
+        x_codes = sb.tile([P, S], U32, align_bytes=64, name="x_codes")
+        x_scales = sb.tile([P, S], U8, align_bytes=64, name="x_scales")
+        for j in range(PACK):
+            nc.vector.tensor_copy(x_bf[:, :, j], x_sb[j][:].indirect(offs_sb[:]))
+        nc.vector.quantize_mx(out=x_codes[:].bitcast(FP8X4), scales=x_scales[:], in_=x_bf[:].rearrange("p c j -> p (c j)"))
+
+        w_bf = sb.tile([P, PACK, P, PACK], BF16, align_bytes=64, name="w_bf")
+        w_dealt = w_bf[:].rearrange("p t m j -> p m t j")
+        nc.scalar.copy(w_dealt[:, 0:64], w_sb[0][:].rearrange("p j (m t) -> p m t j", t=PACK))
+        w_second = w_sb[1][:].rearrange("p j (m t) -> p m t j", t=PACK)
+        nc.scalar.copy(w_dealt[:, 64:88], w_second[:, 0:24])
+        nc.vector.tensor_copy(w_dealt[:, 88:128], w_second[:, 24:64])
+
+        banks = []
+        for t in range(PACK):
+            w_codes = sb.tile([P, P], U32, align_bytes=64, name=f"w_codes{t}")
+            w_scales = sb.tile([P, P], U8, align_bytes=64, name=f"w_scales{t}")
+            nc.vector.quantize_mx(out=w_codes[:].bitcast(FP8X4), scales=w_scales[:], in_=w_bf[:, t].rearrange("p m j -> p (m j)"))
+            bank = psum.tile([P, S], F32, name=f"bank{t}")
+            nc.tensor.matmul_mx(out=bank[:], lhsT=w_codes[:].bitcast(FP8X4), lhsT_scale=w_scales[:],
+                                rhs=x_codes[:].bitcast(FP8X4), rhs_scale=x_scales[:], start=True, stop=True)
+            banks.append(bank)
+
+        o01 = sb.tile([P, 2, S], F32, name="o01")
+        o23 = [sb.tile([P, 2, HALF], F32, name=f"o23_{h}") for h in range(2)]
+        o_bf = [sb.tile([P, HALF, PACK], BF16, align_bytes=64, name=f"o_bf{h}") for h in range(2)]
+        o_codes = [sb.tile([P, HALF], U32, align_bytes=64, name=f"o_codes{h}") for h in range(2)]
+        o_scales = sb.tile([P, S], U8, align_bytes=64, name="o_scales")
+
+        g0 = sb.tile([P, S], F32, name="g0")
+        nc.vector.tensor_copy(g0[:], scale_sb[0][:].indirect(task_sb[:]))
+        nc.vector.tensor_tensor(o01[:, 0, :], banks[0][:], g0[:], MULT)
+        nc.sync.dma_start(out_rows[:, 0, :], o01[:, 0, :])
+
+        y_sb = [None]
+        for t in range(1, PACK):
+            y = sb.tile([P, S], F32, name=f"y{t}")
+            nc.scalar.copy(y[:], banks[t][:])
+            y_sb.append(y)
+
+        nc.vector.tensor_tensor(o01[:, 1, :], scale_sb[1][:].indirect(task_sb[:]), y_sb[1][:], MULT)
+        nc.sync.dma_start(out_rows[:, 1, :], o01[:, 1, :])
+        for h in range(2):
+            cols = slice(h * HALF, (h + 1) * HALF)
+            nc.scalar.copy(o_bf[h][:, :, 0:2], o01[:, :, cols].rearrange("p t c -> p c t"))
+
+        for t in range(2, PACK):
+            for h in range(2):
+                cols = slice(h * HALF, (h + 1) * HALF)
+                entries = task_sb[:, h * HALF // 16 : (h + 1) * HALF // 16]
+                nc.vector.tensor_tensor(o23[h][:, t - 2, :], scale_sb[t][:].indirect(entries), y_sb[t][:, cols], MULT)
+
+        nc.scalar.copy(o_bf[0][:, :, 2:4], o23[0][:].rearrange("p t c -> p c t"))
+        nc.vector.tensor_copy(o_bf[1][:, :, 2:4], o23[1][:].rearrange("p t c -> p c t"))
+        for h in range(2):
+            cols = slice(h * HALF, (h + 1) * HALF)
+            nc.sync.dma_start(out_rows[:, 2:4, cols], o23[h][:])
+        for h in range(2):
+            cols = slice(h * HALF, (h + 1) * HALF)
+            nc.vector.quantize_mx(out=o_codes[h][:].bitcast(FP8X4), scales=o_scales[:, cols], in_=o_bf[h][:].rearrange("p c t -> p (c t)"))
+            nc.sync.dma_start(out_words[:, cols], o_codes[h][:].bitcast(I32))
+        for q in range(4):
+            queue = nc.scalar if q % 2 else nc.sync
+            queue.dma_start(out_scales[4 * q : 4 * q + 4, :], o_scales[32 * q : 32 * q + 4, :].bitcast(I32))

@@ -35,7 +35,7 @@ def tile_picked_none_lo_kernel(tc, xT, w1, scale, offs, task, out_0, out_1, out_
         offs_sb = sb.tile([P, S // 16], U16, name="offs_sb")
         task_sb = sb.tile([P, S // 16], U16, name="task_sb")
         x_sb = [sb.tile([P, T], F32, name=f"x_sb{j}") for j in range(PACK)]
-        w_sb = [sb.tile([P, PACK, N // 2], F32, name=f"w_sb{h}") for h in range(2)]
+        w_sb = [sb.tile([P, PACK, N // 2], F32, name=f"w_sb{h}", tag=f"w_sb{h}") for h in range(2)]
         scale_sb = [sb.tile([P, U], F32, name=f"scale_sb{t}") for t in range(PACK)]
 
         nc.sync.dma_start(x_sb[0][:], x_rows[:, 0, :])
@@ -48,12 +48,16 @@ def tile_picked_none_lo_kernel(tc, xT, w1, scale, offs, task, out_0, out_1, out_
         for t in range(PACK):
             nc.sync.dma_start(scale_sb[t][:], scale_rows[:, t, :])
 
-        x_bf = sb.tile([P, S, PACK], BF16, align_bytes=64, name="x_bf")
         x_codes = sb.tile([P, S], U32, align_bytes=64, name="x_codes")
         x_scales = sb.tile([P, S], U8, align_bytes=64, name="x_scales")
+        x_bf = [sb.tile([P, HALF, PACK], BF16, align_bytes=64, name=f"x_bf{h}") for h in range(2)]
         for j in range(PACK):
-            nc.vector.tensor_copy(x_bf[:, :, j], x_sb[j][:].indirect(offs_sb[:]))
-        nc.vector.quantize_mx(out=x_codes[:].bitcast(FP8X4), scales=x_scales[:], in_=x_bf[:].rearrange("p c j -> p (c j)"))
+            for h in range(2):
+                entries = offs_sb[:, h * HALF // 16 : (h + 1) * HALF // 16]
+                nc.vector.tensor_copy(x_bf[h][:, :, j], x_sb[j][:].indirect(entries))
+        for h in range(2):
+            cols = slice(h * HALF, (h + 1) * HALF)
+            nc.vector.quantize_mx(out=x_codes[:, cols].bitcast(FP8X4), scales=x_scales[:, cols], in_=x_bf[h][:].rearrange("p c j -> p (c j)"))
 
         w_bf = sb.tile([P, PACK, P, PACK], BF16, align_bytes=64, name="w_bf")
         w_dealt = w_bf[:].rearrange("p t m j -> p m t j")
@@ -62,54 +66,63 @@ def tile_picked_none_lo_kernel(tc, xT, w1, scale, offs, task, out_0, out_1, out_
         nc.scalar.copy(w_dealt[:, 64:88], w_second[:, 0:24])
         nc.vector.tensor_copy(w_dealt[:, 88:128], w_second[:, 24:64])
 
-        banks = []
+        def product(t, w_codes, w_scales, cols, name):
+            bank = psum.tile([P, cols.stop - cols.start], F32, name=name)
+            nc.tensor.matmul_mx(out=bank[:], lhsT=w_codes[:].bitcast(FP8X4), lhsT_scale=w_scales[:],
+                                rhs=x_codes[:, cols].bitcast(FP8X4), rhs_scale=x_scales[:, cols], start=True, stop=True)
+            return bank
+
+        y_sb = []
         for t in range(PACK):
             w_codes = sb.tile([P, P], U32, align_bytes=64, name=f"w_codes{t}")
             w_scales = sb.tile([P, P], U8, align_bytes=64, name=f"w_scales{t}")
             nc.vector.quantize_mx(out=w_codes[:].bitcast(FP8X4), scales=w_scales[:], in_=w_bf[:, t].rearrange("p m j -> p (m j)"))
-            bank = psum.tile([P, S], F32, name=f"bank{t}")
-            nc.tensor.matmul_mx(out=bank[:], lhsT=w_codes[:].bitcast(FP8X4), lhsT_scale=w_scales[:],
-                                rhs=x_codes[:].bitcast(FP8X4), rhs_scale=x_scales[:], start=True, stop=True)
-            banks.append(bank)
+            y = sb.tile([P, S], F32, name=f"y{t}")
+            if t == 0:
+                first_bank = product(t, w_codes, w_scales, slice(0, HALF), "bank0a")
+                bank = product(t, w_codes, w_scales, slice(HALF, S), "bank0b")
+                nc.scalar.copy(y[:, HALF:S], bank[:])
+            else:
+                bank = product(t, w_codes, w_scales, slice(0, S), f"bank{t}")
+                nc.scalar.copy(y[:], bank[:])
+            y_sb.append(y)
 
-        o01 = sb.tile([P, 2, S], F32, name="o01")
-        o23 = [sb.tile([P, 2, HALF], F32, name=f"o23_{h}") for h in range(2)]
-        o_bf = [sb.tile([P, HALF, PACK], BF16, align_bytes=64, name=f"o_bf{h}") for h in range(2)]
+        halves = [slice(0, HALF), slice(HALF, S)]
+        chunks = [slice(0, 256), slice(256, 384), slice(384, 512)]
+        o01 = [sb.tile([P, 2, HALF], F32, name=f"o01_{h}") for h in range(2)]
+        o23 = [sb.tile([P, 2, c.stop - c.start], F32, name=f"o23_{c.start}") for c in chunks]
+        o_bf = [sb.tile([P, c.stop - c.start, PACK], BF16, align_bytes=64, name=f"o_bf{c.start}") for c in chunks]
         o_codes = [sb.tile([P, HALF], U32, align_bytes=64, name=f"o_codes{h}") for h in range(2)]
         o_scales = sb.tile([P, S], U8, align_bytes=64, name="o_scales")
 
-        g0 = sb.tile([P, S], F32, name="g0")
-        nc.vector.tensor_copy(g0[:], scale_sb[0][:].indirect(task_sb[:]))
-        nc.vector.tensor_tensor(o01[:, 0, :], banks[0][:], g0[:], MULT)
-        nc.sync.dma_start(out_rows[:, 0, :], o01[:, 0, :])
+        def picked_scale(t, cols):
+            return scale_sb[t][:].indirect(task_sb[:, cols.start // 16 : cols.stop // 16])
 
-        y_sb = [None]
-        for t in range(1, PACK):
-            y = sb.tile([P, S], F32, name=f"y{t}")
-            nc.scalar.copy(y[:], banks[t][:])
-            y_sb.append(y)
-
-        nc.vector.tensor_tensor(o01[:, 1, :], scale_sb[1][:].indirect(task_sb[:]), y_sb[1][:], MULT)
-        nc.sync.dma_start(out_rows[:, 1, :], o01[:, 1, :])
+        g0 = sb.tile([P, HALF], F32, name="g0", tag="w_sb1")
+        nc.vector.tensor_copy(g0[:], picked_scale(0, halves[0]))
+        nc.vector.tensor_tensor(o01[0][:, 0, :], first_bank[:], g0[:], MULT)
+        nc.vector.tensor_tensor(o01[1][:, 0, :], picked_scale(0, halves[1]), y_sb[0][:, halves[1]], MULT)
         for h in range(2):
-            cols = slice(h * HALF, (h + 1) * HALF)
-            nc.scalar.copy(o_bf[h][:, :, 0:2], o01[:, :, cols].rearrange("p t c -> p c t"))
+            nc.vector.tensor_tensor(o01[h][:, 1, :], picked_scale(1, halves[h]), y_sb[1][:, halves[h]], MULT)
+            nc.sync.dma_start(out_rows[:, 0:2, halves[h]], o01[h][:])
+        for i, cols in enumerate(chunks):
+            h = cols.start // HALF
+            part = slice(cols.start - h * HALF, cols.stop - h * HALF)
+            nc.scalar.copy(o_bf[i][:, :, 0:2], o01[h][:, :, part].rearrange("p t c -> p c t"))
 
-        for t in range(2, PACK):
-            for h in range(2):
-                cols = slice(h * HALF, (h + 1) * HALF)
-                entries = task_sb[:, h * HALF // 16 : (h + 1) * HALF // 16]
-                nc.vector.tensor_tensor(o23[h][:, t - 2, :], scale_sb[t][:].indirect(entries), y_sb[t][:, cols], MULT)
-
-        nc.scalar.copy(o_bf[0][:, :, 2:4], o23[0][:].rearrange("p t c -> p c t"))
-        nc.vector.tensor_copy(o_bf[1][:, :, 2:4], o23[1][:].rearrange("p t c -> p c t"))
-        for h in range(2):
-            cols = slice(h * HALF, (h + 1) * HALF)
-            nc.sync.dma_start(out_rows[:, 2:4, cols], o23[h][:])
-        for h in range(2):
-            cols = slice(h * HALF, (h + 1) * HALF)
-            nc.vector.quantize_mx(out=o_codes[h][:].bitcast(FP8X4), scales=o_scales[:, cols], in_=o_bf[h][:].rearrange("p c t -> p (c t)"))
-            nc.sync.dma_start(out_words[:, cols], o_codes[h][:].bitcast(I32))
+        for i, cols in enumerate(chunks):
+            for t in range(2, PACK):
+                nc.vector.tensor_tensor(o23[i][:, t - 2, :], picked_scale(t, cols), y_sb[t][:, cols], MULT)
+            nc.sync.dma_start(out_rows[:, 2:4, cols], o23[i][:])
+        for i, cols in enumerate(chunks):
+            copy = nc.vector.tensor_copy if i == 2 else nc.scalar.copy
+            copy(o_bf[i][:, :, 2:4], o23[i][:].rearrange("p t c -> p c t"))
+        for i, cols in enumerate(chunks):
+            h = cols.start // HALF
+            part = slice(cols.start - h * HALF, cols.stop - h * HALF)
+            nc.vector.quantize_mx(out=o_codes[h][:, part].bitcast(FP8X4), scales=o_scales[:, cols], in_=o_bf[i][:].rearrange("p c t -> p (c t)"))
+            if cols.stop % HALF == 0:
+                nc.sync.dma_start(out_words[:, halves[h]], o_codes[h][:].bitcast(I32))
         for q in range(4):
             queue = nc.scalar if q % 2 else nc.sync
             queue.dma_start(out_scales[4 * q : 4 * q + 4, :], o_scales[32 * q : 32 * q + 4, :].bitcast(I32))

@@ -60,9 +60,9 @@ def tile_picked_none_lo_kernel(tc, xT, w1, scale, offs, task, out_0, out_1, out_
             nc.vector.quantize_mx(out=x_codes[:, cols].bitcast(FP8X4), scales=x_scales[:, cols], in_=x_bf[h][:].rearrange("p c j -> p (c j)"))
 
         w_bf = sb.tile([P, PACK, P, PACK], BF16, align_bytes=64, name="w_bf")
-        w_dealt = w_bf[:].rearrange("p t m j -> p m t j")
-        nc.scalar.copy(w_dealt[:, 0:64], w_sb[0][:].rearrange("p j (m t) -> p m t j", t=PACK))
-        w_second = w_sb[1][:].rearrange("p j (m t) -> p m t j", t=PACK)
+        w_dealt = w_bf[:].rearrange("p t m j -> p m j t")
+        nc.scalar.copy(w_dealt[:, 0:64], w_sb[0][:].rearrange("p j (m t) -> p m j t", t=PACK))
+        w_second = w_sb[1][:].rearrange("p j (m t) -> p m j t", t=PACK)
         nc.scalar.copy(w_dealt[:, 64:88], w_second[:, 0:24])
         nc.vector.tensor_copy(w_dealt[:, 88:128], w_second[:, 24:64])
 
@@ -89,8 +89,7 @@ def tile_picked_none_lo_kernel(tc, xT, w1, scale, offs, task, out_0, out_1, out_
 
         halves = [slice(0, HALF), slice(HALF, S)]
         chunks = [slice(0, 256), slice(256, 384), slice(384, 512)]
-        o01 = [sb.tile([P, 2, HALF], F32, name=f"o01_{h}") for h in range(2)]
-        o23 = [sb.tile([P, 2, c.stop - c.start], F32, name=f"o23_{c.start}") for c in chunks]
+        o_sb = sb.tile([P, PACK, S], F32, name="o_sb")
         o_bf = [sb.tile([P, c.stop - c.start, PACK], BF16, align_bytes=64, name=f"o_bf{c.start}") for c in chunks]
         o_codes = [sb.tile([P, HALF], U32, align_bytes=64, name=f"o_codes{h}") for h in range(2)]
         o_scales = sb.tile([P, S], U8, align_bytes=64, name="o_scales")
@@ -98,25 +97,26 @@ def tile_picked_none_lo_kernel(tc, xT, w1, scale, offs, task, out_0, out_1, out_
         def picked_scale(t, cols):
             return scale_sb[t][:].indirect(task_sb[:, cols.start // 16 : cols.stop // 16])
 
+        def scaled(t, cols):
+            nc.vector.tensor_tensor(o_sb[:, t, cols], picked_scale(t, cols), y_sb[t][:, cols], MULT)
+
         g0 = sb.tile([P, HALF], F32, name="g0", tag="w_sb1")
         nc.vector.tensor_copy(g0[:], picked_scale(0, halves[0]))
-        nc.vector.tensor_tensor(o01[0][:, 0, :], first_bank[:], g0[:], MULT)
-        nc.vector.tensor_tensor(o01[1][:, 0, :], picked_scale(0, halves[1]), y_sb[0][:, halves[1]], MULT)
-        for h in range(2):
-            nc.vector.tensor_tensor(o01[h][:, 1, :], picked_scale(1, halves[h]), y_sb[1][:, halves[h]], MULT)
-            nc.sync.dma_start(out_rows[:, 0:2, halves[h]], o01[h][:])
-        for i, cols in enumerate(chunks):
-            h = cols.start // HALF
-            part = slice(cols.start - h * HALF, cols.stop - h * HALF)
-            nc.scalar.copy(o_bf[i][:, :, 0:2], o01[h][:, :, part].rearrange("p t c -> p c t"))
+        nc.vector.tensor_tensor(o_sb[:, 0, halves[0]], first_bank[:], g0[:], MULT)
+        scaled(0, halves[1])
+        nc.sync.dma_start(out_rows[:, 0, :], o_sb[:, 0, :])
+        scaled(1, slice(0, S))
+        nc.sync.dma_start(out_rows[:, 1, :], o_sb[:, 1, :])
 
         for i, cols in enumerate(chunks):
             for t in range(2, PACK):
-                nc.vector.tensor_tensor(o23[i][:, t - 2, :], picked_scale(t, cols), y_sb[t][:, cols], MULT)
-            nc.sync.dma_start(out_rows[:, 2:4, cols], o23[i][:])
+                scaled(t, cols)
+            if cols.stop % HALF == 0:
+                half = halves[cols.start // HALF]
+                nc.sync.dma_start(out_rows[:, 2:4, half], o_sb[:, 2:4, half])
         for i, cols in enumerate(chunks):
             copy = nc.vector.tensor_copy if i == 2 else nc.scalar.copy
-            copy(o_bf[i][:, :, 2:4], o23[i][:].rearrange("p t c -> p c t"))
+            copy(o_bf[i][:].rearrange("p (c i) t -> p c t i", i=4), o_sb[:, :, cols].rearrange("p t (c i) -> p c t i", i=4))
         for i, cols in enumerate(chunks):
             h = cols.start // HALF
             part = slice(cols.start - h * HALF, cols.stop - h * HALF)

@@ -35,9 +35,9 @@ def tile_picked_none_lo_kernel(tc, xT, w1, scale, offs, task, out_0, out_1, out_
         offs_sb = sb.tile([P, S // 16], U16, name="offs_sb")
         task_sb = sb.tile([P, S // 16], U16, name="task_sb")
         x_sb = [sb.tile([P, T], F32, name=f"x_sb{j}") for j in range(PACK)]
-        w_sb = [sb.tile([P, PACK, N // 2], F32, name=f"w_sb{h}", tag=f"w_sb{h}") for h in range(2)]
         scale_sb = [sb.tile([P, U], F32, name=f"scale_sb{t}") for t in range(PACK)]
-
+        halves = [slice(0, HALF), slice(HALF, S)]
+        w_sb = [sb.tile([P, PACK, N // 2], F32, name=f"w_sb{h}", tag=f"w_sb{h}") for h in range(2)]
         nc.sync.dma_start(x_sb[0][:], x_rows[:, 0, :])
         nc.sync.dma_start(offs_sb[:], offs)
         for j in range(1, PACK):
@@ -50,79 +50,99 @@ def tile_picked_none_lo_kernel(tc, xT, w1, scale, offs, task, out_0, out_1, out_
 
         x_codes = sb.tile([P, S], U32, align_bytes=64, name="x_codes")
         x_scales = sb.tile([P, S], U8, align_bytes=64, name="x_scales")
-        x_bf = [sb.tile([P, HALF, PACK], BF16, align_bytes=64, name=f"x_bf{h}") for h in range(2)]
+        x_bf = sb.tile([P, S, PACK], BF16, align_bytes=64, name="x_bf")
         for j in range(PACK):
-            for h in range(2):
-                entries = offs_sb[:, h * HALF // 16 : (h + 1) * HALF // 16]
-                nc.vector.tensor_copy(x_bf[h][:, :, j], x_sb[j][:].indirect(entries))
-        for h in range(2):
-            cols = slice(h * HALF, (h + 1) * HALF)
-            nc.vector.quantize_mx(out=x_codes[:, cols].bitcast(FP8X4), scales=x_scales[:, cols], in_=x_bf[h][:].rearrange("p c j -> p (c j)"))
+            nc.vector.tensor_copy(x_bf[:, :, j], x_sb[j][:].indirect(offs_sb[:]))
+        nc.vector.quantize_mx(out=x_codes[:].bitcast(FP8X4), scales=x_scales[:], in_=x_bf[:].rearrange("p c j -> p (c j)"))
 
-        w_bf = sb.tile([P, PACK, P, PACK], BF16, align_bytes=64, name="w_bf")
-        w_dealt = w_bf[:].rearrange("p t m j -> p m j t")
-        nc.scalar.copy(w_dealt[:, 0:64], w_sb[0][:].rearrange("p j (m t) -> p m j t", t=PACK))
-        w_second = w_sb[1][:].rearrange("p j (m t) -> p m j t", t=PACK)
-        nc.scalar.copy(w_dealt[:, 64:88], w_second[:, 0:24])
-        nc.vector.tensor_copy(w_dealt[:, 88:128], w_second[:, 24:64])
+        w_bf = [sb.tile([P, 2, P, PACK], BF16, align_bytes=64, name=f"w_bf{u}") for u in range(2)]
 
-        def product(t, w_codes, w_scales, cols, name):
-            bank = psum.tile([P, cols.stop - cols.start], F32, name=name)
-            nc.tensor.matmul_mx(out=bank[:], lhsT=w_codes[:].bitcast(FP8X4), lhsT_scale=w_scales[:],
+        def dealt(copy, h, u):
+            copy(w_bf[u][:, :, 64 * h : 64 * h + 64, :].rearrange("p t m j -> p m j t"),
+                 w_sb[h][:].rearrange("p j (m t) -> p m j t", t=PACK)[:, :, :, 2 * u : 2 * u + 2])
+
+        dealt(nc.scalar.copy, 0, 0)
+        dealt(nc.scalar.copy, 0, 1)
+        dealt(nc.vector.tensor_copy, 1, 0)
+        dealt(nc.scalar.copy, 1, 1)
+
+        def product(out, w_codes, w_scales, cols):
+            nc.tensor.matmul_mx(out=out, lhsT=w_codes.bitcast(FP8X4), lhsT_scale=w_scales,
                                 rhs=x_codes[:, cols].bitcast(FP8X4), rhs_scale=x_scales[:, cols], start=True, stop=True)
-            return bank
 
-        y_sb = []
-        for t in range(PACK):
-            w_codes = sb.tile([P, P], U32, align_bytes=64, name=f"w_codes{t}")
-            w_scales = sb.tile([P, P], U8, align_bytes=64, name=f"w_scales{t}")
-            nc.vector.quantize_mx(out=w_codes[:].bitcast(FP8X4), scales=w_scales[:], in_=w_bf[:, t].rearrange("p m j -> p (m j)"))
-            y = sb.tile([P, S], F32, name=f"y{t}")
-            if t == 0:
-                first_bank = product(t, w_codes, w_scales, slice(0, HALF), "bank0a")
-                bank = product(t, w_codes, w_scales, slice(HALF, S), "bank0b")
-                nc.scalar.copy(y[:, HALF:S], bank[:])
-            else:
-                bank = product(t, w_codes, w_scales, slice(0, S), f"bank{t}")
-                nc.scalar.copy(y[:], bank[:])
-            y_sb.append(y)
-
-        halves = [slice(0, HALF), slice(HALF, S)]
-        chunks = [slice(0, 256), slice(256, 384), slice(384, 512)]
-        o_sb = sb.tile([P, PACK, S], F32, name="o_sb")
-        o_bf = [sb.tile([P, c.stop - c.start, PACK], BF16, align_bytes=64, name=f"o_bf{c.start}") for c in chunks]
-        o_codes = [sb.tile([P, HALF], U32, align_bytes=64, name=f"o_codes{h}") for h in range(2)]
-        o_scales = sb.tile([P, S], U8, align_bytes=64, name="o_scales")
+        y_sb = [sb.tile([P, S], F32, name=f"y{t}") for t in range(PACK - 1)]
+        o_sb = sb.tile([P, PACK + 1, S], F32, name="o_sb")
+        y_last = o_sb[:, 2:5:2, HALF:S]
+        for planes in (range(0, 1), range(1, 2), range(2, 4)):
+            w_codes = sb.tile([P, len(planes) * P], U32, align_bytes=64, name=f"w_codes{planes.start}")
+            w_scales = sb.tile([P, len(planes) * P], U8, align_bytes=64, name=f"w_scales{planes.start}")
+            nc.vector.quantize_mx(out=w_codes[:].bitcast(FP8X4), scales=w_scales[:],
+                                  in_=w_bf[planes.start // 2][:, planes.start % 2 : planes.start % 2 + len(planes)].rearrange("p t m j -> p (t m j)"))
+            for t in planes:
+                mine = slice((t - planes.start) * P, (t - planes.start + 1) * P)
+                cols = slice(0, S)
+                if t == 0:
+                    first_bank = psum.tile([P, HALF], F32, name="first_bank")
+                    product(first_bank[:], w_codes[:, mine], w_scales[:, mine], halves[0])
+                    cols = halves[1]
+                bank = psum.tile([P, cols.stop - cols.start], F32, name=f"bank{t}")
+                product(bank[:], w_codes[:, mine], w_scales[:, mine], cols)
+                if t < PACK - 1:
+                    nc.scalar.copy(y_sb[t][:, cols], bank[:])
+                else:
+                    nc.scalar.copy(y_last, bank[:].rearrange("p (h c) -> p h c", h=2))
 
         def picked_scale(t, cols):
             return scale_sb[t][:].indirect(task_sb[:, cols.start // 16 : cols.stop // 16])
 
         def scaled(t, cols):
-            nc.vector.tensor_tensor(o_sb[:, t, cols], picked_scale(t, cols), y_sb[t][:, cols], MULT)
+            h = cols.start // HALF
+            y = y_sb[t][:, cols] if t < PACK - 1 else y_last[:, h, cols.start - h * HALF : cols.stop - h * HALF]
+            nc.vector.tensor_tensor(o_sb[:, t, cols], picked_scale(t, cols), y, MULT)
 
         g0 = sb.tile([P, HALF], F32, name="g0", tag="w_sb1")
         nc.vector.tensor_copy(g0[:], picked_scale(0, halves[0]))
         nc.vector.tensor_tensor(o_sb[:, 0, halves[0]], first_bank[:], g0[:], MULT)
         scaled(0, halves[1])
         nc.sync.dma_start(out_rows[:, 0, :], o_sb[:, 0, :])
-        scaled(1, slice(0, S))
-        nc.sync.dma_start(out_rows[:, 1, :], o_sb[:, 1, :])
 
-        for i, cols in enumerate(chunks):
-            for t in range(2, PACK):
-                scaled(t, cols)
-            if cols.stop % HALF == 0:
-                half = halves[cols.start // HALF]
-                nc.sync.dma_start(out_rows[:, 2:4, half], o_sb[:, 2:4, half])
-        for i, cols in enumerate(chunks):
-            copy = nc.vector.tensor_copy if i == 2 else nc.scalar.copy
-            copy(o_bf[i][:].rearrange("p (c i) t -> p c t i", i=4), o_sb[:, :, cols].rearrange("p t (c i) -> p c t i", i=4))
-        for i, cols in enumerate(chunks):
+        o_bf = [sb.tile([P, HALF, PACK], BF16, align_bytes=64, name=f"o_bf{h}") for h in range(2)]
+        o_codes = [sb.tile([P, HALF], U32, align_bytes=64, name=f"o_codes{h}") for h in range(2)]
+        o_scales = sb.tile([P, S], U8, align_bytes=64, name="o_scales")
+
+        def rounded(copy, cols, planes=slice(0, PACK)):
             h = cols.start // HALF
             part = slice(cols.start - h * HALF, cols.stop - h * HALF)
-            nc.vector.quantize_mx(out=o_codes[h][:, part].bitcast(FP8X4), scales=o_scales[:, cols], in_=o_bf[i][:].rearrange("p c t -> p (c t)"))
+            copy(o_bf[h][:, part, planes].rearrange("p (c i) t -> p c t i", i=4),
+                 o_sb[:, planes, cols].rearrange("p t (c i) -> p c t i", i=4))
+
+        def quantised(cols):
+            h = cols.start // HALF
+            part = slice(cols.start - h * HALF, cols.stop - h * HALF)
+            nc.vector.quantize_mx(out=o_codes[h][:, part].bitcast(FP8X4), scales=o_scales[:, cols],
+                                  in_=o_bf[h][:, part].rearrange("p c t -> p (c t)"))
             if cols.stop % HALF == 0:
                 nc.sync.dma_start(out_words[:, halves[h]], o_codes[h][:].bitcast(I32))
+
+        def stored(planes, cols):
+            nc.sync.dma_start(out_rows[:, planes, cols], o_sb[:, planes, cols])
+
+        chunks = [slice(0, 256), slice(256, 384), slice(384, 512)]
+        for cols in halves:
+            scaled(1, cols)
+            rounded(nc.scalar.copy, cols, slice(0, 2))
+        nc.sync.dma_start(out_rows[:, 1, :], o_sb[:, 1, :])
+        for t in range(2, PACK):
+            scaled(t, halves[0])
+        stored(slice(2, 4), halves[0])
+        rounded(nc.scalar.copy, halves[0], slice(2, 4))
+        scaled(3, halves[1])
+        for cols in chunks[1:]:
+            scaled(2, cols)
+            rounded(nc.scalar.copy, cols, slice(2, 4))
+        stored(slice(2, 4), halves[1])
+        for cols in chunks:
+            quantised(cols)
         for q in range(4):
             queue = nc.scalar if q % 2 else nc.sync
             queue.dma_start(out_scales[4 * q : 4 * q + 4, :], o_scales[32 * q : 32 * q + 4, :].bitcast(I32))

@@ -37,34 +37,40 @@ def tile_picked_none_lo_kernel(tc, xT, w1, scale, offs, task, out_0, out_1, out_
         x_sb = [sb.tile([P, T], F32, name=f"x_sb{j}") for j in range(PACK)]
         scale_sb = [sb.tile([P, U], F32, name=f"scale_sb{t}") for t in range(PACK)]
         halves = [slice(0, HALF), slice(HALF, S)]
-        w_sb = [sb.tile([P, PACK, N // 2], F32, name=f"w_sb{h}", tag=f"w_sb{h}") for h in range(2)]
+        w_cols = [slice(0, 192), slice(192, N)]
+        w_sb = [sb.tile([P, PACK, c.stop - c.start], F32, name=f"w_sb{c.start}") for c in w_cols]
         nc.sync.dma_start(x_sb[0][:], x_rows[:, 0, :])
         nc.sync.dma_start(offs_sb[:], offs)
         for j in range(1, PACK):
             nc.sync.dma_start(x_sb[j][:], x_rows[:, j, :])
         for h in range(2):
-            nc.sync.dma_start(w_sb[h][:], w_rows[:, :, h * (N // 2) : (h + 1) * (N // 2)])
+            nc.sync.dma_start(w_sb[h][:], w_rows[:, :, w_cols[h]])
         nc.sync.dma_start(task_sb[:], task)
         for t in range(PACK):
             nc.sync.dma_start(scale_sb[t][:], scale_rows[:, t, :])
 
+        x_bf = sb.tile([P, S, PACK], BF16, align_bytes=64, name="x_bf")
+        for j in range(PACK - 1):
+            nc.vector.tensor_copy(x_bf[:, :, j], x_sb[j][:].indirect(offs_sb[:]))
         x_codes = sb.tile([P, S], U32, align_bytes=64, name="x_codes")
         x_scales = sb.tile([P, S], U8, align_bytes=64, name="x_scales")
-        x_bf = sb.tile([P, S, PACK], BF16, align_bytes=64, name="x_bf")
-        for j in range(PACK):
-            nc.vector.tensor_copy(x_bf[:, :, j], x_sb[j][:].indirect(offs_sb[:]))
-        nc.vector.quantize_mx(out=x_codes[:].bitcast(FP8X4), scales=x_scales[:], in_=x_bf[:].rearrange("p c j -> p (c j)"))
+        for cols in halves:
+            nc.vector.tensor_copy(x_bf[:, cols, PACK - 1], x_sb[PACK - 1][:].indirect(offs_sb[:, cols.start // 16 : cols.stop // 16]))
+            nc.vector.quantize_mx(out=x_codes[:, cols].bitcast(FP8X4), scales=x_scales[:, cols],
+                                  in_=x_bf[:, cols].rearrange("p c j -> p (c j)"))
 
-        w_bf = [sb.tile([P, 2, P, PACK], BF16, align_bytes=64, name=f"w_bf{u}") for u in range(2)]
+        w_bf = [sb.tile([P, 2, P, PACK], BF16, align_bytes=64, name=f"w_bf{u}", tag=f"w_bf{u}") for u in range(2)]
 
-        def dealt(copy, h, u):
-            copy(w_bf[u][:, :, 64 * h : 64 * h + 64, :].rearrange("p t m j -> p m j t"),
-                 w_sb[h][:].rearrange("p j (m t) -> p m j t", t=PACK)[:, :, :, 2 * u : 2 * u + 2])
+        def dealt(copy, h, u, groups):
+            first = w_cols[h].start // PACK
+            copy(w_bf[u][:, :, groups, :].rearrange("p t m j -> p m j t"),
+                 w_sb[h][:].rearrange("p j (m t) -> p m j t", t=PACK)[:, groups.start - first : groups.stop - first, :, 2 * u : 2 * u + 2])
 
-        dealt(nc.scalar.copy, 0, 0)
-        dealt(nc.scalar.copy, 0, 1)
-        dealt(nc.vector.tensor_copy, 1, 0)
-        dealt(nc.scalar.copy, 1, 1)
+        dealt(nc.scalar.copy, 0, 0, slice(0, 48))
+        dealt(nc.scalar.copy, 0, 1, slice(0, 48))
+        dealt(nc.scalar.copy, 1, 0, slice(48, 92))
+        dealt(nc.vector.tensor_copy, 1, 0, slice(92, P))
+        dealt(nc.scalar.copy, 1, 1, slice(48, P))
 
         def product(out, w_codes, w_scales, cols):
             nc.tensor.matmul_mx(out=out, lhsT=w_codes.bitcast(FP8X4), lhsT_scale=w_scales,
@@ -100,7 +106,7 @@ def tile_picked_none_lo_kernel(tc, xT, w1, scale, offs, task, out_0, out_1, out_
             y = y_sb[t][:, cols] if t < PACK - 1 else y_last[:, h, cols.start - h * HALF : cols.stop - h * HALF]
             nc.vector.tensor_tensor(o_sb[:, t, cols], picked_scale(t, cols), y, MULT)
 
-        g0 = sb.tile([P, HALF], F32, name="g0", tag="w_sb1")
+        g0 = sb.tile([P, HALF], F32, align_bytes=64, name="g0", tag="w_bf0")
         nc.vector.tensor_copy(g0[:], picked_scale(0, halves[0]))
         nc.vector.tensor_tensor(o_sb[:, 0, halves[0]], first_bank[:], g0[:], MULT)
         scaled(0, halves[1])

@@ -13,6 +13,7 @@ U16 = mybir.dt.uint16
 U8 = mybir.dt.uint8
 FP8X4 = mybir.dt.float8_e4m3fn_x4
 MULT = mybir.AluOpType.mult
+ADD = mybir.AluOpType.add
 
 P = 128
 PACK = 4
@@ -37,7 +38,7 @@ def tile_picked_none_lo_kernel(tc, xT, w1, scale, offs, task, out_0, out_1, out_
         x_sb = [sb.tile([P, T], F32, name=f"x_sb{j}") for j in range(PACK)]
         scale_sb = [sb.tile([P, U], F32, name=f"scale_sb{t}") for t in range(PACK)]
         halves = [slice(0, HALF), slice(HALF, S)]
-        w_cols = [slice(0, 192), slice(192, N)]
+        w_cols = [slice(0, 256), slice(256, N)]
         w_sb = [sb.tile([P, PACK, c.stop - c.start], F32, name=f"w_sb{c.start}") for c in w_cols]
         nc.sync.dma_start(x_sb[0][:], x_rows[:, 0, :])
         nc.sync.dma_start(offs_sb[:], offs)
@@ -66,11 +67,12 @@ def tile_picked_none_lo_kernel(tc, xT, w1, scale, offs, task, out_0, out_1, out_
             copy(w_bf[u][:, :, groups, :].rearrange("p t m j -> p m j t"),
                  w_sb[h][:].rearrange("p j (m t) -> p m j t", t=PACK)[:, groups.start - first : groups.stop - first, :, 2 * u : 2 * u + 2])
 
-        dealt(nc.scalar.copy, 0, 0, slice(0, 48))
-        dealt(nc.scalar.copy, 0, 1, slice(0, 48))
-        dealt(nc.scalar.copy, 1, 0, slice(48, 92))
-        dealt(nc.vector.tensor_copy, 1, 0, slice(92, P))
-        dealt(nc.scalar.copy, 1, 1, slice(48, P))
+        dealt(nc.scalar.copy, 0, 0, slice(0, 64))
+        nc.gpsimd.tensor_scalar(w_bf[1][:, :, 0:40, :], w_sb[0][:].rearrange("p j (m t) -> p t m j", t=PACK)[:, 2:4, 0:40], 1.0, 0.0, MULT, ADD)
+        dealt(nc.scalar.copy, 0, 1, slice(40, 64))
+        dealt(nc.scalar.copy, 1, 0, slice(64, 100))
+        dealt(nc.vector.tensor_copy, 1, 0, slice(100, P))
+        dealt(nc.scalar.copy, 1, 1, slice(64, P))
 
         def product(out, w_codes, w_scales, cols):
             nc.tensor.matmul_mx(out=out, lhsT=w_codes.bitcast(FP8X4), lhsT_scale=w_scales,
@@ -79,6 +81,7 @@ def tile_picked_none_lo_kernel(tc, xT, w1, scale, offs, task, out_0, out_1, out_
         y_sb = [sb.tile([P, S], F32, name=f"y{t}") for t in range(PACK - 1)]
         o_sb = sb.tile([P, PACK + 1, S], F32, name="o_sb")
         y_last = o_sb[:, 2:5:2, HALF:S]
+        ramp = [slice(0, 128), slice(128, 256), slice(256, 512)]
         for planes in (range(0, 1), range(1, 2), range(2, 4)):
             w_codes = sb.tile([P, len(planes) * P], U32, align_bytes=64, name=f"w_codes{planes.start}")
             w_scales = sb.tile([P, len(planes) * P], U8, align_bytes=64, name=f"w_scales{planes.start}")
@@ -86,17 +89,15 @@ def tile_picked_none_lo_kernel(tc, xT, w1, scale, offs, task, out_0, out_1, out_
                                   in_=w_bf[planes.start // 2][:, planes.start % 2 : planes.start % 2 + len(planes)].rearrange("p t m j -> p (t m j)"))
             for t in planes:
                 mine = slice((t - planes.start) * P, (t - planes.start + 1) * P)
-                cols = slice(0, S)
-                if t == 0:
-                    first_bank = psum.tile([P, HALF], F32, name="first_bank")
-                    product(first_bank[:], w_codes[:, mine], w_scales[:, mine], halves[0])
-                    cols = halves[1]
-                bank = psum.tile([P, cols.stop - cols.start], F32, name=f"bank{t}")
-                product(bank[:], w_codes[:, mine], w_scales[:, mine], cols)
-                if t < PACK - 1:
-                    nc.scalar.copy(y_sb[t][:, cols], bank[:])
-                else:
-                    nc.scalar.copy(y_last, bank[:].rearrange("p (h c) -> p h c", h=2))
+                for cols in [ramp, halves, [slice(0, S)], [slice(0, S)]][t]:
+                    bank = psum.tile([P, cols.stop - cols.start], F32, name=f"bank{t}_{cols.start}")
+                    product(bank[:], w_codes[:, mine], w_scales[:, mine], cols)
+                    if t == 0 and cols.start == 0:
+                        first_bank = bank
+                    elif t < PACK - 1:
+                        nc.scalar.copy(y_sb[t][:, cols], bank[:])
+                    else:
+                        nc.scalar.copy(y_last, bank[:].rearrange("p (h c) -> p h c", h=2))
 
         def picked_scale(t, cols):
             return scale_sb[t][:].indirect(task_sb[:, cols.start // 16 : cols.stop // 16])
@@ -106,10 +107,11 @@ def tile_picked_none_lo_kernel(tc, xT, w1, scale, offs, task, out_0, out_1, out_
             y = y_sb[t][:, cols] if t < PACK - 1 else y_last[:, h, cols.start - h * HALF : cols.stop - h * HALF]
             nc.vector.tensor_tensor(o_sb[:, t, cols], picked_scale(t, cols), y, MULT)
 
-        g0 = sb.tile([P, HALF], F32, align_bytes=64, name="g0", tag="w_bf0")
-        nc.vector.tensor_copy(g0[:], picked_scale(0, halves[0]))
-        nc.vector.tensor_tensor(o_sb[:, 0, halves[0]], first_bank[:], g0[:], MULT)
-        scaled(0, halves[1])
+        g0 = sb.tile([P, 128], F32, align_bytes=64, name="g0", tag="w_bf0")
+        nc.vector.tensor_copy(g0[:], picked_scale(0, ramp[0]))
+        nc.vector.tensor_tensor(o_sb[:, 0, ramp[0]], first_bank[:], g0[:], MULT)
+        for cols in ramp[1:]:
+            scaled(0, cols)
         nc.sync.dma_start(out_rows[:, 0, :], o_sb[:, 0, :])
 
         o_bf = [sb.tile([P, HALF, PACK], BF16, align_bytes=64, name=f"o_bf{h}") for h in range(2)]

@@ -14,6 +14,7 @@ U8 = mybir.dt.uint8
 FP8X4 = mybir.dt.float8_e4m3fn_x4
 MULT = mybir.AluOpType.mult
 ADD = mybir.AluOpType.add
+COPY = mybir.ActivationFunctionType.Copy
 
 P = 128
 PACK = 4
@@ -62,13 +63,15 @@ def tile_picked_none_lo_kernel(tc, xT, w1, scale, offs, task, out_0, out_1, out_
 
         w_bf = [sb.tile([P, 2, P, PACK], BF16, align_bytes=64, name=f"w_bf{u}", tag=f"w_bf{u}") for u in range(2)]
 
+        pairs = [slice(0, 4, 3), slice(1, 3)]
+
         def dealt(copy, h, u, groups):
             first = w_cols[h].start // PACK
             copy(w_bf[u][:, :, groups, :].rearrange("p t m j -> p m j t"),
-                 w_sb[h][:].rearrange("p j (m t) -> p m j t", t=PACK)[:, groups.start - first : groups.stop - first, :, 2 * u : 2 * u + 2])
+                 w_sb[h][:].rearrange("p j (m t) -> p m j t", t=PACK)[:, groups.start - first : groups.stop - first, :, pairs[u]])
 
         dealt(nc.scalar.copy, 0, 0, slice(0, 64))
-        nc.gpsimd.tensor_scalar(w_bf[1][:, :, 0:40, :], w_sb[0][:].rearrange("p j (m t) -> p t m j", t=PACK)[:, 2:4, 0:40], 1.0, 0.0, MULT, ADD)
+        nc.gpsimd.tensor_scalar(w_bf[1][:, :, 0:40, :], w_sb[0][:].rearrange("p j (m t) -> p t m j", t=PACK)[:, pairs[1], 0:40], 1.0, 0.0, MULT, ADD)
         dealt(nc.scalar.copy, 0, 1, slice(40, 64))
         dealt(nc.scalar.copy, 1, 0, slice(64, 100))
         dealt(nc.vector.tensor_copy, 1, 0, slice(100, P))
@@ -78,78 +81,98 @@ def tile_picked_none_lo_kernel(tc, xT, w1, scale, offs, task, out_0, out_1, out_
             nc.tensor.matmul_mx(out=out, lhsT=w_codes.bitcast(FP8X4), lhsT_scale=w_scales,
                                 rhs=x_codes[:, cols].bitcast(FP8X4), rhs_scale=x_scales[:, cols], start=True, stop=True)
 
-        y_sb = [sb.tile([P, S], F32, name=f"y{t}") for t in range(PACK - 1)]
-        o_sb = sb.tile([P, PACK + 1, S], F32, name="o_sb")
-        y_last = o_sb[:, 2:5:2, HALF:S]
-        ramp = [slice(0, 128), slice(128, 256), slice(256, 512)]
-        for planes in (range(0, 1), range(1, 2), range(2, 4)):
-            w_codes = sb.tile([P, len(planes) * P], U32, align_bytes=64, name=f"w_codes{planes.start}")
-            w_scales = sb.tile([P, len(planes) * P], U8, align_bytes=64, name=f"w_scales{planes.start}")
+        banks = {}
+
+        def quantised_w(u, slots):
+            w_codes = sb.tile([P, len(slots) * P], U32, align_bytes=64, name=f"w_codes{u}_{slots.start}")
+            w_scales = sb.tile([P, len(slots) * P], U8, align_bytes=64, name=f"w_scales{u}_{slots.start}")
             nc.vector.quantize_mx(out=w_codes[:].bitcast(FP8X4), scales=w_scales[:],
-                                  in_=w_bf[planes.start // 2][:, planes.start % 2 : planes.start % 2 + len(planes)].rearrange("p t m j -> p (t m j)"))
-            for t in planes:
-                mine = slice((t - planes.start) * P, (t - planes.start + 1) * P)
-                for cols in [ramp, halves, [slice(0, S)], [slice(0, S)]][t]:
-                    bank = psum.tile([P, cols.stop - cols.start], F32, name=f"bank{t}_{cols.start}")
-                    product(bank[:], w_codes[:, mine], w_scales[:, mine], cols)
-                    if t == 0 and cols.start == 0:
-                        first_bank = bank
-                    elif t < PACK - 1:
-                        nc.scalar.copy(y_sb[t][:, cols], bank[:])
-                    else:
-                        nc.scalar.copy(y_last, bank[:].rearrange("p (h c) -> p h c", h=2))
+                                  in_=w_bf[u][:, slots.start : slots.stop].rearrange("p t m j -> p (t m j)"))
+            return [(w_codes[:, i * P : (i + 1) * P], w_scales[:, i * P : (i + 1) * P]) for i in range(len(slots))]
 
-        def picked_scale(t, cols):
-            return scale_sb[t][:].indirect(task_sb[:, cols.start // 16 : cols.stop // 16])
+        def multiplied(t, cols):
+            bank = psum.tile([P, cols.stop - cols.start], F32, name=f"bank{t}_{cols.start}")
+            product(bank[:], *w_mx[t], cols)
+            for c in range(cols.start, cols.stop, 128):
+                banks[t, c] = (bank, cols.start)
 
-        def scaled(t, cols):
-            h = cols.start // HALF
-            y = y_sb[t][:, cols] if t < PACK - 1 else y_last[:, h, cols.start - h * HALF : cols.stop - h * HALF]
-            nc.vector.tensor_tensor(o_sb[:, t, cols], picked_scale(t, cols), y, MULT)
+        whole = slice(0, S)
+        w_mx = {}
+        (w_mx[0],) = quantised_w(0, range(0, 1))
+        multiplied(0, halves[0])
+        multiplied(0, halves[1])
+        (w_mx[3],) = quantised_w(0, range(1, 2))
+        multiplied(3, halves[0])
+        w_mx[1], w_mx[2] = quantised_w(1, range(0, 2))
+        multiplied(1, whole)
+        multiplied(2, whole)
+        multiplied(3, halves[1])
 
-        g0 = sb.tile([P, 128], F32, align_bytes=64, name="g0", tag="w_bf0")
-        nc.vector.tensor_copy(g0[:], picked_scale(0, ramp[0]))
-        nc.vector.tensor_tensor(o_sb[:, 0, ramp[0]], first_bank[:], g0[:], MULT)
-        for cols in ramp[1:]:
-            scaled(0, cols)
-        nc.sync.dma_start(out_rows[:, 0, :], o_sb[:, 0, :])
-
+        g_sb = [sb.tile([P, S], F32, name=f"g{t}") for t in range(PACK)]
+        y_sb = sb.tile([P, HALF], F32, name="y_sb")
+        o_sb = sb.tile([P, PACK, S], F32, name="o_sb")
         o_bf = [sb.tile([P, HALF, PACK], BF16, align_bytes=64, name=f"o_bf{h}") for h in range(2)]
         o_codes = [sb.tile([P, HALF], U32, align_bytes=64, name=f"o_codes{h}") for h in range(2)]
         o_scales = sb.tile([P, S], U8, align_bytes=64, name="o_scales")
 
-        def rounded(copy, cols, planes=slice(0, PACK)):
+        def window(t, cols):
+            return scale_sb[t][:].indirect(task_sb[:, cols.start // 16 : cols.stop // 16])
+
+        def in_half(cols):
             h = cols.start // HALF
-            part = slice(cols.start - h * HALF, cols.stop - h * HALF)
+            return h, slice(cols.start - h * HALF, cols.stop - h * HALF)
+
+        def picked_by_scalar(t, cols):
+            nc.scalar.activation(g_sb[t][:, cols], window(t, cols), COPY)
+
+        def picked_by_vector(t, cols):
+            nc.vector.tensor_copy(g_sb[t][:, cols], window(t, cols))
+
+        def sums(t, cols):
+            bank, first = banks[t, cols.start]
+            return bank[:, cols.start - first : cols.stop - first]
+
+        def scaled(t, cols):
+            nc.vector.tensor_tensor(o_sb[:, t, cols], sums(t, cols), g_sb[t][:, cols], MULT)
+
+        def rounded(copy, cols, planes=slice(0, PACK)):
+            h, part = in_half(cols)
             copy(o_bf[h][:, part, planes].rearrange("p (c i) t -> p c t i", i=4),
                  o_sb[:, planes, cols].rearrange("p t (c i) -> p c t i", i=4))
 
         def quantised(cols):
-            h = cols.start // HALF
-            part = slice(cols.start - h * HALF, cols.stop - h * HALF)
+            h, part = in_half(cols)
             nc.vector.quantize_mx(out=o_codes[h][:, part].bitcast(FP8X4), scales=o_scales[:, cols],
                                   in_=o_bf[h][:, part].rearrange("p c t -> p (c t)"))
             if cols.stop % HALF == 0:
                 nc.sync.dma_start(out_words[:, halves[h]], o_codes[h][:].bitcast(I32))
 
-        def stored(planes, cols):
-            nc.sync.dma_start(out_rows[:, planes, cols], o_sb[:, planes, cols])
+        def stored(t, cols=slice(0, S)):
+            nc.sync.dma_start(out_rows[:, t, cols], o_sb[:, t, cols])
 
-        chunks = [slice(0, 256), slice(256, 384), slice(384, 512)]
+        chunks = [slice(c, c + 128) for c in range(0, S, 128)]
+        picked_by_vector(0, halves[0])
+        picked_by_scalar(0, halves[1])
+        nc.scalar.copy(y_sb[:], sums(3, halves[0]))
         for cols in halves:
-            scaled(1, cols)
-            rounded(nc.scalar.copy, cols, slice(0, 2))
-        nc.sync.dma_start(out_rows[:, 1, :], o_sb[:, 1, :])
-        for t in range(2, PACK):
-            scaled(t, halves[0])
-        stored(slice(2, 4), halves[0])
-        rounded(nc.scalar.copy, halves[0], slice(2, 4))
+            scaled(0, cols)
+        stored(0)
+        for t in (1, 2):
+            picked_by_scalar(t, halves[0])
+            picked_by_scalar(t, chunks[2])
+            picked_by_vector(t, chunks[3])
+            for cols in halves:
+                scaled(t, cols)
+            stored(t)
+        picked_by_scalar(3, halves[1])
+        nc.vector.tensor_tensor(o_sb[:, 3, halves[0]], window(3, halves[0]), y_sb[:], MULT)
         scaled(3, halves[1])
-        for cols in chunks[1:]:
-            scaled(2, cols)
-            rounded(nc.scalar.copy, cols, slice(2, 4))
-        stored(slice(2, 4), halves[1])
-        for cols in chunks:
+        stored(3)
+        rounded(nc.scalar.copy, chunks[0])
+        rounded(nc.vector.tensor_copy, chunks[1])
+        rounded(nc.vector.tensor_copy, chunks[2])
+        rounded(nc.scalar.copy, chunks[3])
+        for cols in halves:
             quantised(cols)
         for q in range(4):
             queue = nc.scalar if q % 2 else nc.sync

@@ -98,10 +98,8 @@ def tile_picked_none_lo_kernel(tc, xT, w1, scale, offs, task, out_0, out_1, out_
 
         whole = slice(0, S)
         w_mx = {}
-        (w_mx[0],) = quantised_w(0, range(0, 1))
-        multiplied(0, halves[0])
-        multiplied(0, halves[1])
-        (w_mx[3],) = quantised_w(0, range(1, 2))
+        w_mx[0], w_mx[3] = quantised_w(0, range(0, 2))
+        multiplied(0, whole)
         multiplied(3, halves[0])
         w_mx[1], w_mx[2] = quantised_w(1, range(0, 2))
         multiplied(1, whole)
@@ -109,8 +107,8 @@ def tile_picked_none_lo_kernel(tc, xT, w1, scale, offs, task, out_0, out_1, out_
         multiplied(3, halves[1])
 
         g_sb = [sb.tile([P, S], F32, name=f"g{t}") for t in range(PACK)]
-        y_sb = sb.tile([P, HALF], F32, name="y_sb")
         o_sb = sb.tile([P, PACK, S], F32, name="o_sb")
+        y_sb = o_sb[:, 2, halves[1]]
         o_bf = [sb.tile([P, HALF, PACK], BF16, align_bytes=64, name=f"o_bf{h}") for h in range(2)]
         o_codes = [sb.tile([P, HALF], U32, align_bytes=64, name=f"o_codes{h}") for h in range(2)]
         o_scales = sb.tile([P, S], U8, align_bytes=64, name="o_scales")
@@ -153,27 +151,26 @@ def tile_picked_none_lo_kernel(tc, xT, w1, scale, offs, task, out_0, out_1, out_
         chunks = [slice(c, c + 128) for c in range(0, S, 128)]
         picked_by_vector(0, halves[0])
         picked_by_scalar(0, halves[1])
-        nc.scalar.copy(y_sb[:], sums(3, halves[0]))
-        for cols in halves:
-            scaled(0, cols)
+        nc.scalar.copy(y_sb, sums(3, halves[0]))
+        scaled(0, whole)
         stored(0)
-        for t in (1, 2):
-            picked_by_scalar(t, halves[0])
-            picked_by_scalar(t, chunks[2])
-            picked_by_vector(t, chunks[3])
-            for cols in halves:
-                scaled(t, cols)
-            stored(t)
+        picked_by_scalar(1, slice(0, 320))
+        picked_by_vector(1, slice(320, S))
+        scaled(1, whole)
+        stored(1)
+        for cols in halves:
+            picked_by_scalar(2, cols)
+        scaled(2, halves[0])
         picked_by_scalar(3, halves[1])
-        nc.vector.tensor_tensor(o_sb[:, 3, halves[0]], window(3, halves[0]), y_sb[:], MULT)
+        nc.vector.tensor_tensor(o_sb[:, 3, halves[0]], window(3, halves[0]), y_sb, MULT)
+        scaled(2, halves[1])
+        stored(2)
         scaled(3, halves[1])
         stored(3)
-        rounded(nc.scalar.copy, chunks[0])
-        rounded(nc.vector.tensor_copy, chunks[1])
-        rounded(nc.vector.tensor_copy, chunks[2])
-        rounded(nc.scalar.copy, chunks[3])
-        for cols in halves:
-            quantised(cols)
+        rounded(nc.scalar.copy, halves[0])
+        rounded(nc.vector.tensor_copy, halves[1])
+        quantised(halves[0])
+        quantised(halves[1])
         for q in range(4):
             queue = nc.scalar if q % 2 else nc.sync
             queue.dma_start(out_scales[4 * q : 4 * q + 4, :], o_scales[32 * q : 32 * q + 4, :].bitcast(I32))

@@ -37,7 +37,7 @@ def tile_picked_none_lo_kernel(tc, xT, w1, scale, offs, task, out_0, out_1, out_
         offs_sb = sb.tile([P, S // 16], U16, name="offs_sb")
         task_sb = sb.tile([P, S // 16], U16, name="task_sb")
         x_sb = [sb.tile([P, T], F32, name=f"x_sb{j}") for j in range(PACK)]
-        scale_sb = [sb.tile([P, U], F32, name=f"scale_sb{t}") for t in range(PACK)]
+        scale_sb = [sb.tile([P, U], F32, name=f"scale_sb{t}", tag=f"scale_sb{t}") for t in range(PACK)]
         halves = [slice(0, HALF), slice(HALF, S)]
         w_cols = [slice(0, 256), slice(256, N)]
         w_sb = [sb.tile([P, PACK, c.stop - c.start], F32, name=f"w_sb{c.start}") for c in w_cols]
@@ -98,17 +98,19 @@ def tile_picked_none_lo_kernel(tc, xT, w1, scale, offs, task, out_0, out_1, out_
 
         whole = slice(0, S)
         w_mx = {}
-        w_mx[0], w_mx[3] = quantised_w(0, range(0, 2))
-        multiplied(0, whole)
+        (w_mx[3],) = quantised_w(0, range(1, 2))
         multiplied(3, halves[0])
+        (w_mx[0],) = quantised_w(0, range(0, 1))
+        multiplied(0, whole)
         w_mx[1], w_mx[2] = quantised_w(1, range(0, 2))
         multiplied(1, whole)
-        multiplied(2, whole)
-        multiplied(3, halves[1])
+        multiplied(2, halves[0])
+        last_bank = psum.tile([P, 2, HALF], F32, name="last_bank")
+        for t in (2, 3):
+            product(last_bank[:, t - 2, :], *w_mx[t], halves[1])
 
-        g_sb = [sb.tile([P, S], F32, name=f"g{t}") for t in range(PACK)]
+        g_sb = sb.tile([P, PACK, S], F32, name="g_sb")
         o_sb = sb.tile([P, PACK, S], F32, name="o_sb")
-        y_sb = o_sb[:, 2, halves[1]]
         o_bf = [sb.tile([P, HALF, PACK], BF16, align_bytes=64, name=f"o_bf{h}") for h in range(2)]
         o_codes = [sb.tile([P, HALF], U32, align_bytes=64, name=f"o_codes{h}") for h in range(2)]
         o_scales = sb.tile([P, S], U8, align_bytes=64, name="o_scales")
@@ -121,17 +123,17 @@ def tile_picked_none_lo_kernel(tc, xT, w1, scale, offs, task, out_0, out_1, out_
             return h, slice(cols.start - h * HALF, cols.stop - h * HALF)
 
         def picked_by_scalar(t, cols):
-            nc.scalar.activation(g_sb[t][:, cols], window(t, cols), COPY)
+            nc.scalar.activation(g_sb[:, t, cols], window(t, cols), COPY)
 
         def picked_by_vector(t, cols):
-            nc.vector.tensor_copy(g_sb[t][:, cols], window(t, cols))
+            nc.vector.tensor_copy(g_sb[:, t, cols], window(t, cols))
 
         def sums(t, cols):
             bank, first = banks[t, cols.start]
             return bank[:, cols.start - first : cols.stop - first]
 
         def scaled(t, cols):
-            nc.vector.tensor_tensor(o_sb[:, t, cols], sums(t, cols), g_sb[t][:, cols], MULT)
+            nc.vector.tensor_tensor(o_sb[:, t, cols], sums(t, cols), g_sb[:, t, cols], MULT)
 
         def rounded(copy, cols, planes=slice(0, PACK)):
             h, part = in_half(cols)
@@ -151,24 +153,25 @@ def tile_picked_none_lo_kernel(tc, xT, w1, scale, offs, task, out_0, out_1, out_
         chunks = [slice(c, c + 128) for c in range(0, S, 128)]
         picked_by_vector(0, halves[0])
         picked_by_scalar(0, halves[1])
-        nc.scalar.copy(y_sb, sums(3, halves[0]))
+        y_sb = sb.tile([P, HALF], F32, name="y_sb", tag="scale_sb0")
+        nc.scalar.copy(y_sb[:], sums(3, halves[0]))
         scaled(0, whole)
         stored(0)
-        picked_by_scalar(1, slice(0, 320))
-        picked_by_vector(1, slice(320, S))
+        picked_by_scalar(1, slice(0, 352))
+        picked_by_vector(1, slice(352, S))
         scaled(1, whole)
         stored(1)
         for cols in halves:
             picked_by_scalar(2, cols)
         scaled(2, halves[0])
         picked_by_scalar(3, halves[1])
-        nc.vector.tensor_tensor(o_sb[:, 3, halves[0]], window(3, halves[0]), y_sb, MULT)
-        scaled(2, halves[1])
-        stored(2)
-        scaled(3, halves[1])
-        stored(3)
+        nc.vector.tensor_tensor(o_sb[:, 3, halves[0]], window(3, halves[0]), y_sb[:], MULT)
+        stored(slice(2, 4), halves[0])
+        nc.vector.tensor_tensor(o_sb[:, 2:4, halves[1]], last_bank[:], g_sb[:, 2:4, halves[1]], MULT)
+        stored(slice(2, 4), halves[1])
         rounded(nc.scalar.copy, halves[0])
-        rounded(nc.vector.tensor_copy, halves[1])
+        rounded(nc.vector.tensor_copy, slice(HALF, 448))
+        rounded(nc.scalar.copy, slice(448, S))
         quantised(halves[0])
         quantised(halves[1])
         for q in range(4):

@@ -19,6 +19,12 @@ COPY = mybir.ActivationFunctionType.Copy
 P = 128
 PACK = 4
 HALF = S // 2
+STRIPE = 16
+HALF_GROUPS = P // 2
+GPSIMD_GROUPS = 40
+SCALAR_GROUPS = 36
+SCALAR_PICKS = 352
+SCALAR_ROUNDS = 64
 
 
 def tile_picked_none_lo_kernel(tc, xT, w1, scale, offs, task, out_0, out_1, out_2):
@@ -29,27 +35,30 @@ def tile_picked_none_lo_kernel(tc, xT, w1, scale, offs, task, out_0, out_1, out_
     out_rows = out_0.rearrange("(p t) c -> p t c", t=PACK)
     out_words = out_1[0].rearrange("p c r -> p (c r)").bitcast(I32)
     out_scales = out_2[0].bitcast(I32)
+    halves = [slice(0, HALF), slice(HALF, S)]
+    whole = slice(0, S)
 
     with ExitStack() as ctx:
         sb = ctx.enter_context(tc.tile_pool(name="sb", bufs=1))
         psum = ctx.enter_context(tc.psum_pool(name="psum", bufs=1))
 
-        offs_sb = sb.tile([P, S // 16], U16, name="offs_sb")
-        task_sb = sb.tile([P, S // 16], U16, name="task_sb")
+        offs_sb = sb.tile([P, S // STRIPE], U16, name="offs_sb")
+        task_sb = sb.tile([P, S // STRIPE], U16, name="task_sb")
         x_sb = [sb.tile([P, T], F32, name=f"x_sb{j}") for j in range(PACK)]
         scale_sb = [sb.tile([P, U], F32, name=f"scale_sb{t}", tag=f"scale_sb{t}") for t in range(PACK)]
-        halves = [slice(0, HALF), slice(HALF, S)]
-        w_cols = [slice(0, 256), slice(256, N)]
-        w_sb = [sb.tile([P, PACK, c.stop - c.start], F32, name=f"w_sb{c.start}") for c in w_cols]
+        w_sb = [sb.tile([P, PACK, N // 2], F32, name=f"w_sb{h}") for h in range(2)]
         nc.sync.dma_start(x_sb[0][:], x_rows[:, 0, :])
         nc.sync.dma_start(offs_sb[:], offs)
         for j in range(1, PACK):
             nc.sync.dma_start(x_sb[j][:], x_rows[:, j, :])
         for h in range(2):
-            nc.sync.dma_start(w_sb[h][:], w_rows[:, :, w_cols[h]])
+            nc.sync.dma_start(w_sb[h][:], w_rows[:, :, h * N // 2 : (h + 1) * N // 2])
         nc.sync.dma_start(task_sb[:], task)
         for t in range(PACK):
             nc.sync.dma_start(scale_sb[t][:], scale_rows[:, t, :])
+
+        def entries(list_sb, cols):
+            return list_sb[:, cols.start // STRIPE : cols.stop // STRIPE]
 
         x_bf = sb.tile([P, S, PACK], BF16, align_bytes=64, name="x_bf")
         for j in range(PACK - 1):
@@ -57,57 +66,54 @@ def tile_picked_none_lo_kernel(tc, xT, w1, scale, offs, task, out_0, out_1, out_
         x_codes = sb.tile([P, S], U32, align_bytes=64, name="x_codes")
         x_scales = sb.tile([P, S], U8, align_bytes=64, name="x_scales")
         for cols in halves:
-            nc.vector.tensor_copy(x_bf[:, cols, PACK - 1], x_sb[PACK - 1][:].indirect(offs_sb[:, cols.start // 16 : cols.stop // 16]))
+            nc.vector.tensor_copy(x_bf[:, cols, PACK - 1], x_sb[PACK - 1][:].indirect(entries(offs_sb, cols)))
             nc.vector.quantize_mx(out=x_codes[:, cols].bitcast(FP8X4), scales=x_scales[:, cols],
                                   in_=x_bf[:, cols].rearrange("p c j -> p (c j)"))
 
-        w_bf = [sb.tile([P, 2, P, PACK], BF16, align_bytes=64, name=f"w_bf{u}", tag=f"w_bf{u}") for u in range(2)]
-
+        w_bf = [sb.tile([P, 2, P, PACK], BF16, align_bytes=64, name=f"w_bf{u}") for u in range(2)]
         pairs = [slice(0, 4, 3), slice(1, 3)]
 
-        def dealt(copy, h, u, groups):
-            first = w_cols[h].start // PACK
-            copy(w_bf[u][:, :, groups, :].rearrange("p t m j -> p m j t"),
-                 w_sb[h][:].rearrange("p j (m t) -> p m j t", t=PACK)[:, groups.start - first : groups.stop - first, :, pairs[u]])
+        def dealt(copy, h, u, first, last):
+            groups = slice(h * HALF_GROUPS + first, h * HALF_GROUPS + last)
+            copy(w_bf[u][:, :, groups, :].rearrange("p i g j -> p g j i"),
+                 w_sb[h][:].rearrange("p j (g t) -> p g j t", t=PACK)[:, first:last, :, pairs[u]])
 
-        dealt(nc.scalar.copy, 0, 0, slice(0, 64))
-        nc.gpsimd.tensor_scalar(w_bf[1][:, :, 0:40, :], w_sb[0][:].rearrange("p j (m t) -> p t m j", t=PACK)[:, pairs[1], 0:40], 1.0, 0.0, MULT, ADD)
-        dealt(nc.scalar.copy, 0, 1, slice(40, 64))
-        dealt(nc.scalar.copy, 1, 0, slice(64, 100))
-        dealt(nc.vector.tensor_copy, 1, 0, slice(100, P))
-        dealt(nc.scalar.copy, 1, 1, slice(64, P))
+        dealt(nc.scalar.copy, 0, 0, 0, HALF_GROUPS)
+        nc.gpsimd.tensor_scalar(w_bf[1][:, :, 0:GPSIMD_GROUPS, :],
+                                w_sb[0][:].rearrange("p j (g t) -> p t g j", t=PACK)[:, pairs[1], 0:GPSIMD_GROUPS],
+                                1.0, 0.0, MULT, ADD)
+        dealt(nc.scalar.copy, 0, 1, GPSIMD_GROUPS, HALF_GROUPS)
+        dealt(nc.scalar.copy, 1, 0, 0, SCALAR_GROUPS)
+        dealt(nc.vector.tensor_copy, 1, 0, SCALAR_GROUPS, HALF_GROUPS)
+        dealt(nc.scalar.copy, 1, 1, 0, HALF_GROUPS)
 
-        def product(out, w_codes, w_scales, cols):
-            nc.tensor.matmul_mx(out=out, lhsT=w_codes.bitcast(FP8X4), lhsT_scale=w_scales,
+        def quantised_w(u, first, last):
+            count = last - first
+            codes = sb.tile([P, count * P], U32, align_bytes=64, name=f"w_codes{u}_{first}")
+            scales = sb.tile([P, count * P], U8, align_bytes=64, name=f"w_scales{u}_{first}")
+            nc.vector.quantize_mx(out=codes[:].bitcast(FP8X4), scales=scales[:],
+                                  in_=w_bf[u][:, first:last].rearrange("p i g j -> p (i g j)"))
+            return [(codes[:, i * P : (i + 1) * P], scales[:, i * P : (i + 1) * P]) for i in range(count)]
+
+        def product(out, w_plane, cols):
+            codes, scales = w_plane
+            nc.tensor.matmul_mx(out=out, lhsT=codes.bitcast(FP8X4), lhsT_scale=scales,
                                 rhs=x_codes[:, cols].bitcast(FP8X4), rhs_scale=x_scales[:, cols], start=True, stop=True)
 
-        banks = {}
-
-        def quantised_w(u, slots):
-            w_codes = sb.tile([P, len(slots) * P], U32, align_bytes=64, name=f"w_codes{u}_{slots.start}")
-            w_scales = sb.tile([P, len(slots) * P], U8, align_bytes=64, name=f"w_scales{u}_{slots.start}")
-            nc.vector.quantize_mx(out=w_codes[:].bitcast(FP8X4), scales=w_scales[:],
-                                  in_=w_bf[u][:, slots.start : slots.stop].rearrange("p t m j -> p (t m j)"))
-            return [(w_codes[:, i * P : (i + 1) * P], w_scales[:, i * P : (i + 1) * P]) for i in range(len(slots))]
-
-        def multiplied(t, cols):
-            bank = psum.tile([P, cols.stop - cols.start], F32, name=f"bank{t}_{cols.start}")
-            product(bank[:], *w_mx[t], cols)
-            for c in range(cols.start, cols.stop, 128):
-                banks[t, c] = (bank, cols.start)
-
-        whole = slice(0, S)
-        w_mx = {}
-        (w_mx[3],) = quantised_w(0, range(1, 2))
-        multiplied(3, halves[0])
-        (w_mx[0],) = quantised_w(0, range(0, 1))
-        multiplied(0, whole)
-        w_mx[1], w_mx[2] = quantised_w(1, range(0, 2))
-        multiplied(1, whole)
-        multiplied(2, halves[0])
-        last_bank = psum.tile([P, 2, HALF], F32, name="last_bank")
-        for t in (2, 3):
-            product(last_bank[:, t - 2, :], *w_mx[t], halves[1])
+        (w_plane3,) = quantised_w(0, 1, 2)
+        sums3_first = psum.tile([P, HALF], F32, name="sums3_first")
+        product(sums3_first[:], w_plane3, halves[0])
+        (w_plane0,) = quantised_w(0, 0, 1)
+        sums0 = psum.tile([P, S], F32, name="sums0")
+        product(sums0[:], w_plane0, whole)
+        w_plane1, w_plane2 = quantised_w(1, 0, 2)
+        sums1 = psum.tile([P, S], F32, name="sums1")
+        product(sums1[:], w_plane1, whole)
+        sums2_first = psum.tile([P, HALF], F32, name="sums2_first")
+        product(sums2_first[:], w_plane2, halves[0])
+        sums23_second = psum.tile([P, 2, HALF], F32, name="sums23_second")
+        product(sums23_second[:, 0, :], w_plane2, halves[1])
+        product(sums23_second[:, 1, :], w_plane3, halves[1])
 
         g_sb = sb.tile([P, PACK, S], F32, name="g_sb")
         o_sb = sb.tile([P, PACK, S], F32, name="o_sb")
@@ -116,11 +122,7 @@ def tile_picked_none_lo_kernel(tc, xT, w1, scale, offs, task, out_0, out_1, out_
         o_scales = sb.tile([P, S], U8, align_bytes=64, name="o_scales")
 
         def window(t, cols):
-            return scale_sb[t][:].indirect(task_sb[:, cols.start // 16 : cols.stop // 16])
-
-        def in_half(cols):
-            h = cols.start // HALF
-            return h, slice(cols.start - h * HALF, cols.stop - h * HALF)
+            return scale_sb[t][:].indirect(entries(task_sb, cols))
 
         def picked_by_scalar(t, cols):
             nc.scalar.activation(g_sb[:, t, cols], window(t, cols), COPY)
@@ -128,52 +130,52 @@ def tile_picked_none_lo_kernel(tc, xT, w1, scale, offs, task, out_0, out_1, out_
         def picked_by_vector(t, cols):
             nc.vector.tensor_copy(g_sb[:, t, cols], window(t, cols))
 
-        def sums(t, cols):
-            bank, first = banks[t, cols.start]
-            return bank[:, cols.start - first : cols.stop - first]
+        def scaled(planes, cols, sums):
+            nc.vector.tensor_tensor(o_sb[:, planes, cols], sums, g_sb[:, planes, cols], MULT)
 
-        def scaled(t, cols):
-            nc.vector.tensor_tensor(o_sb[:, t, cols], sums(t, cols), g_sb[:, t, cols], MULT)
+        def stored(planes, cols):
+            nc.sync.dma_start(out_rows[:, planes, cols], o_sb[:, planes, cols])
 
-        def rounded(copy, cols, planes=slice(0, PACK)):
-            h, part = in_half(cols)
-            copy(o_bf[h][:, part, planes].rearrange("p (c i) t -> p c t i", i=4),
-                 o_sb[:, planes, cols].rearrange("p t (c i) -> p c t i", i=4))
-
-        def quantised(cols):
-            h, part = in_half(cols)
-            nc.vector.quantize_mx(out=o_codes[h][:, part].bitcast(FP8X4), scales=o_scales[:, cols],
-                                  in_=o_bf[h][:, part].rearrange("p c t -> p (c t)"))
-            if cols.stop % HALF == 0:
-                nc.sync.dma_start(out_words[:, halves[h]], o_codes[h][:].bitcast(I32))
-
-        def stored(t, cols=slice(0, S)):
-            nc.sync.dma_start(out_rows[:, t, cols], o_sb[:, t, cols])
-
-        chunks = [slice(c, c + 128) for c in range(0, S, 128)]
         picked_by_vector(0, halves[0])
         picked_by_scalar(0, halves[1])
-        y_sb = sb.tile([P, HALF], F32, name="y_sb", tag="scale_sb0")
-        nc.scalar.copy(y_sb[:], sums(3, halves[0]))
-        scaled(0, whole)
-        stored(0)
-        picked_by_scalar(1, slice(0, 352))
-        picked_by_vector(1, slice(352, S))
-        scaled(1, whole)
-        stored(1)
+        y3_first = sb.tile([P, HALF], F32, name="y3_first", tag="scale_sb0")
+        nc.scalar.copy(y3_first[:], sums3_first[:])
+        scaled(0, whole, sums0[:])
+        stored(0, whole)
+
+        picked_by_scalar(1, halves[0])
+        picked_by_scalar(1, slice(HALF, SCALAR_PICKS))
+        picked_by_vector(1, slice(SCALAR_PICKS, S))
+        for cols in halves:
+            scaled(1, cols, sums1[:, cols])
+        stored(1, whole)
+
+        last_pair = slice(2, 4)
         for cols in halves:
             picked_by_scalar(2, cols)
-        scaled(2, halves[0])
+        scaled(2, halves[0], sums2_first[:])
         picked_by_scalar(3, halves[1])
-        nc.vector.tensor_tensor(o_sb[:, 3, halves[0]], window(3, halves[0]), y_sb[:], MULT)
-        stored(slice(2, 4), halves[0])
-        nc.vector.tensor_tensor(o_sb[:, 2:4, halves[1]], last_bank[:], g_sb[:, 2:4, halves[1]], MULT)
-        stored(slice(2, 4), halves[1])
-        rounded(nc.scalar.copy, halves[0])
-        rounded(nc.vector.tensor_copy, slice(HALF, 448))
-        rounded(nc.scalar.copy, slice(448, S))
-        quantised(halves[0])
-        quantised(halves[1])
+        nc.vector.tensor_tensor(o_sb[:, 3, halves[0]], window(3, halves[0]), y3_first[:], MULT)
+        stored(last_pair, halves[0])
+        quarters = [slice(HALF, HALF + S // 4), slice(HALF + S // 4, S)]
+        for cols in quarters:
+            scaled(last_pair, cols, sums23_second[:, :, cols.start - HALF : cols.stop - HALF])
+        stored(last_pair, halves[1])
+
+        def rounded(copy, h, cols):
+            part = slice(cols.start - h * HALF, cols.stop - h * HALF)
+            copy(o_bf[h][:, part, :].rearrange("p (c i) t -> p c t i", i=4),
+                 o_sb[:, :, cols].rearrange("p t (c i) -> p c t i", i=4))
+
+        rounded(nc.scalar.copy, 0, halves[0])
+        rounded(nc.vector.tensor_copy, 1, quarters[0])
+        rounded(nc.vector.tensor_copy, 1, slice(quarters[1].start, S - SCALAR_ROUNDS))
+        rounded(nc.scalar.copy, 1, slice(S - SCALAR_ROUNDS, S))
+        for h, cols in enumerate(halves):
+            nc.vector.quantize_mx(out=o_codes[h][:].bitcast(FP8X4), scales=o_scales[:, cols],
+                                  in_=o_bf[h][:].rearrange("p c t -> p (c t)"))
+            nc.sync.dma_start(out_words[:, cols], o_codes[h][:].bitcast(I32))
+
         for q in range(4):
             queue = nc.scalar if q % 2 else nc.sync
             queue.dma_start(out_scales[4 * q : 4 * q + 4, :], o_scales[32 * q : 32 * q + 4, :].bitcast(I32))

@@ -104,8 +104,9 @@ def tile_picked_none_lo_kernel(tc, xT, w1, scale, offs, task, out_0, out_1, out_
         sums3_first = psum.tile([P, HALF], F32, name="sums3_first")
         product(sums3_first[:], w_plane3, halves[0])
         (w_plane0,) = quantised_w(0, 0, 1)
-        sums0 = psum.tile([P, S], F32, name="sums0")
-        product(sums0[:], w_plane0, whole)
+        sums0 = [psum.tile([P, HALF], F32, name=f"sums0_{h}") for h in range(2)]
+        for h, cols in enumerate(halves):
+            product(sums0[h][:], w_plane0, cols)
         w_plane1, w_plane2 = quantised_w(1, 0, 2)
         sums1 = psum.tile([P, S], F32, name="sums1")
         product(sums1[:], w_plane1, whole)
@@ -140,7 +141,8 @@ def tile_picked_none_lo_kernel(tc, xT, w1, scale, offs, task, out_0, out_1, out_
         picked_by_scalar(0, halves[1])
         y3_first = sb.tile([P, HALF], F32, name="y3_first", tag="scale_sb0")
         nc.scalar.copy(y3_first[:], sums3_first[:])
-        scaled(0, whole, sums0[:])
+        for h, cols in enumerate(halves):
+            scaled(0, cols, sums0[h][:])
         stored(0, whole)
 
         picked_by_scalar(1, halves[0])
@@ -155,7 +157,9 @@ def tile_picked_none_lo_kernel(tc, xT, w1, scale, offs, task, out_0, out_1, out_
             picked_by_scalar(2, cols)
         scaled(2, halves[0], sums2_first[:])
         picked_by_scalar(3, halves[1])
-        nc.vector.tensor_tensor(o_sb[:, 3, halves[0]], window(3, halves[0]), y3_first[:], MULT)
+        first_quarters = [slice(0, S // 4), slice(S // 4, HALF)]
+        for cols in first_quarters:
+            nc.vector.tensor_tensor(o_sb[:, 3, cols], window(3, cols), y3_first[:, cols], MULT)
         stored(last_pair, halves[0])
         quarters = [slice(HALF, HALF + S // 4), slice(HALF + S // 4, S)]
         for cols in quarters:
@@ -167,7 +171,8 @@ def tile_picked_none_lo_kernel(tc, xT, w1, scale, offs, task, out_0, out_1, out_
             copy(o_bf[h][:, part, :].rearrange("p (c i) t -> p c t i", i=4),
                  o_sb[:, :, cols].rearrange("p t (c i) -> p c t i", i=4))
 
-        rounded(nc.scalar.copy, 0, halves[0])
+        for cols in first_quarters:
+            rounded(nc.scalar.copy, 0, cols)
         rounded(nc.vector.tensor_copy, 1, quarters[0])
         rounded(nc.vector.tensor_copy, 1, slice(quarters[1].start, S - SCALAR_ROUNDS))
         rounded(nc.scalar.copy, 1, slice(S - SCALAR_ROUNDS, S))

@@ -168,8 +168,8 @@ def tile_picked_none_lo_kernel(tc, xT, w1, scale, offs, task, out_0, out_1, out_
 
         def rounded(copy, h, cols):
             part = slice(cols.start - h * HALF, cols.stop - h * HALF)
-            copy(o_bf[h][:, part, :].rearrange("p (c i) t -> p c t i", i=4),
-                 o_sb[:, :, cols].rearrange("p t (c i) -> p c t i", i=4))
+            copy(o_bf[h][:, part, :].rearrange("p (c i) t -> p c t i", i=2),
+                 o_sb[:, :, cols].rearrange("p t (c i) -> p c t i", i=2))
 
         for cols in first_quarters:
             rounded(nc.scalar.copy, 0, cols)

@@ -20,9 +20,8 @@ P = 128
 PACK = 4
 HALF = S // 2
 STRIPE = 16
-HALF_GROUPS = P // 2
-GPSIMD_GROUPS = 40
-SCALAR_GROUPS = 36
+GPSIMD_GROUPS = 80
+SCALAR_GROUPS = 48
 SCALAR_PICKS = 352
 SCALAR_ROUNDS = 64
 
@@ -46,13 +45,13 @@ def tile_picked_none_lo_kernel(tc, xT, w1, scale, offs, task, out_0, out_1, out_
         task_sb = sb.tile([P, S // STRIPE], U16, name="task_sb")
         x_sb = [sb.tile([P, T], F32, name=f"x_sb{j}") for j in range(PACK)]
         scale_sb = [sb.tile([P, U], F32, name=f"scale_sb{t}", tag=f"scale_sb{t}") for t in range(PACK)]
-        w_sb = [sb.tile([P, PACK, N // 2], F32, name=f"w_sb{h}") for h in range(2)]
+        w_sb = [sb.tile([P, 2, N], F32, name=f"w_sb{h}") for h in range(2)]
         nc.sync.dma_start(x_sb[0][:], x_rows[:, 0, :])
         nc.sync.dma_start(offs_sb[:], offs)
         for j in range(1, PACK):
             nc.sync.dma_start(x_sb[j][:], x_rows[:, j, :])
         for h in range(2):
-            nc.sync.dma_start(w_sb[h][:], w_rows[:, :, h * N // 2 : (h + 1) * N // 2])
+            nc.sync.dma_start(w_sb[h][:], w_rows[:, 2 * h : 2 * h + 2, :])
         nc.sync.dma_start(task_sb[:], task)
         for t in range(PACK):
             nc.sync.dma_start(scale_sb[t][:], scale_rows[:, t, :])
@@ -74,18 +73,18 @@ def tile_picked_none_lo_kernel(tc, xT, w1, scale, offs, task, out_0, out_1, out_
         pairs = [slice(0, 4, 3), slice(1, 3)]
 
         def dealt(copy, h, u, first, last):
-            groups = slice(h * HALF_GROUPS + first, h * HALF_GROUPS + last)
-            copy(w_bf[u][:, :, groups, :].rearrange("p i g j -> p g j i"),
-                 w_sb[h][:].rearrange("p j (g t) -> p g j t", t=PACK)[:, first:last, :, pairs[u]])
+            copy(w_bf[u][:, :, first:last, 2 * h : 2 * h + 2].rearrange("p i (c e) j -> p c i e j", e=2),
+                 w_sb[h][:].rearrange("p j (c e t) -> p c t e j", e=2, t=PACK)[:, first // 2 : last // 2, pairs[u]])
 
-        dealt(nc.scalar.copy, 0, 0, 0, HALF_GROUPS)
-        nc.gpsimd.tensor_scalar(w_bf[1][:, :, 0:GPSIMD_GROUPS, :],
+        dealt(nc.scalar.copy, 0, 0, 0, P)
+        nc.gpsimd.tensor_scalar(w_bf[1][:, :, 0:GPSIMD_GROUPS, 0:2],
                                 w_sb[0][:].rearrange("p j (g t) -> p t g j", t=PACK)[:, pairs[1], 0:GPSIMD_GROUPS],
                                 1.0, 0.0, MULT, ADD)
-        dealt(nc.scalar.copy, 0, 1, GPSIMD_GROUPS, HALF_GROUPS)
+        dealt(nc.scalar.copy, 0, 1, GPSIMD_GROUPS, P)
         dealt(nc.scalar.copy, 1, 0, 0, SCALAR_GROUPS)
-        dealt(nc.vector.tensor_copy, 1, 0, SCALAR_GROUPS, HALF_GROUPS)
-        dealt(nc.scalar.copy, 1, 1, 0, HALF_GROUPS)
+        dealt(nc.vector.tensor_copy, 1, 0, SCALAR_GROUPS, P)
+        dealt(nc.vector.tensor_copy, 1, 1, GPSIMD_GROUPS, P)
+        dealt(nc.scalar.copy, 1, 1, 0, GPSIMD_GROUPS)
 
         def quantised_w(u, first, last):
             count = last - first

@@ -13,15 +13,13 @@ U16 = mybir.dt.uint16
 U8 = mybir.dt.uint8
 FP8X4 = mybir.dt.float8_e4m3fn_x4
 MULT = mybir.AluOpType.mult
-ADD = mybir.AluOpType.add
 COPY = mybir.ActivationFunctionType.Copy
 
 P = 128
 PACK = 4
 HALF = S // 2
 STRIPE = 16
-GPSIMD_GROUPS = 80
-SCALAR_GROUPS = 48
+SCALAR_GROUPS = 64
 SCALAR_PICKS = 352
 SCALAR_ROUNDS = 64
 
@@ -76,15 +74,11 @@ def tile_picked_none_lo_kernel(tc, xT, w1, scale, offs, task, out_0, out_1, out_
             copy(w_bf[u][:, :, first:last, 2 * h : 2 * h + 2].rearrange("p i (c e) j -> p c i e j", e=2),
                  w_sb[h][:].rearrange("p j (c e t) -> p c t e j", e=2, t=PACK)[:, first // 2 : last // 2, pairs[u]])
 
-        dealt(nc.scalar.copy, 0, 0, 0, P)
-        nc.gpsimd.tensor_scalar(w_bf[1][:, :, 0:GPSIMD_GROUPS, 0:2],
-                                w_sb[0][:].rearrange("p j (g t) -> p t g j", t=PACK)[:, pairs[1], 0:GPSIMD_GROUPS],
-                                1.0, 0.0, MULT, ADD)
-        dealt(nc.scalar.copy, 0, 1, GPSIMD_GROUPS, P)
-        dealt(nc.scalar.copy, 1, 0, 0, SCALAR_GROUPS)
-        dealt(nc.vector.tensor_copy, 1, 0, SCALAR_GROUPS, P)
-        dealt(nc.vector.tensor_copy, 1, 1, GPSIMD_GROUPS, P)
-        dealt(nc.scalar.copy, 1, 1, 0, GPSIMD_GROUPS)
+        for u in range(2):
+            dealt(nc.scalar.copy, 0, u, 0, P)
+        dealt(nc.vector.tensor_copy, 1, 0, 0, P)
+        dealt(nc.vector.tensor_copy, 1, 1, SCALAR_GROUPS, P)
+        dealt(nc.scalar.copy, 1, 1, 0, SCALAR_GROUPS)
 
         def quantised_w(u, first, last):
             count = last - first

@@ -20,7 +20,6 @@ PACK = 4
 HALF = S // 2
 STRIPE = 16
 SCALAR_GROUPS = 64
-SCALAR_PICKS = 352
 SCALAR_ROUNDS = 64
 
 
@@ -139,8 +138,7 @@ def tile_picked_none_lo_kernel(tc, xT, w1, scale, offs, task, out_0, out_1, out_
         stored(0, whole)
 
         picked_by_scalar(1, halves[0])
-        picked_by_scalar(1, slice(HALF, SCALAR_PICKS))
-        picked_by_vector(1, slice(SCALAR_PICKS, S))
+        picked_by_vector(1, halves[1])
         for cols in halves:
             scaled(1, cols, sums1[:, cols])
         stored(1, whole)

from contextlib import ExitStack

import concourse.mybir as mybir

K, T, S, N, U = 512, 2048, 512, 512, 1024
FLOPS = 2 * K * N * S

F32 = mybir.dt.float32
BF16 = mybir.dt.bfloat16
I32 = mybir.dt.int32
U32 = mybir.dt.uint32
U16 = mybir.dt.uint16
U8 = mybir.dt.uint8
FP8X4 = mybir.dt.float8_e4m3fn_x4
MULT = mybir.AluOpType.mult
COPY = mybir.ActivationFunctionType.Copy

P = 128
PACK = 4
HALF = S // 2
STRIPE = 16
SCALAR_GROUPS = 64
SCALAR_ROUNDS = 64


def tile_picked_none_lo_kernel(tc, xT, w1, scale, offs, task, out_0, out_1, out_2):
    nc = tc.nc
    x_rows = xT.rearrange("(p j) c -> p j c", j=PACK)
    w_rows = w1.rearrange("(p j) c -> p j c", j=PACK)
    scale_rows = scale.rearrange("(p t) c -> p t c", t=PACK)
    out_rows = out_0.rearrange("(p t) c -> p t c", t=PACK)
    out_words = out_1[0].rearrange("p c r -> p (c r)").bitcast(I32)
    out_scales = out_2[0].bitcast(I32)
    halves = [slice(0, HALF), slice(HALF, S)]
    whole = slice(0, S)

    with ExitStack() as ctx:
        sb = ctx.enter_context(tc.tile_pool(name="sb", bufs=1))
        psum = ctx.enter_context(tc.psum_pool(name="psum", bufs=1))

        offs_sb = sb.tile([P, S // STRIPE], U16, name="offs_sb")
        task_sb = sb.tile([P, S // STRIPE], U16, name="task_sb")
        x_sb = [sb.tile([P, T], F32, name=f"x_sb{j}") for j in range(PACK)]
        scale_sb = [sb.tile([P, U], F32, name=f"scale_sb{t}", tag=f"scale_sb{t}") for t in range(PACK)]
        w_sb = [sb.tile([P, 2, N], F32, name=f"w_sb{h}") for h in range(2)]
        nc.sync.dma_start(x_sb[0][:], x_rows[:, 0, :])
        nc.sync.dma_start(offs_sb[:], offs)
        for j in range(1, PACK):
            nc.sync.dma_start(x_sb[j][:], x_rows[:, j, :])
        for h in range(2):
            nc.sync.dma_start(w_sb[h][:], w_rows[:, 2 * h : 2 * h + 2, :])
        nc.sync.dma_start(task_sb[:], task)
        for t in range(PACK):
            nc.sync.dma_start(scale_sb[t][:], scale_rows[:, t, :])

        def entries(list_sb, cols):
            return list_sb[:, cols.start // STRIPE : cols.stop // STRIPE]

        x_bf = sb.tile([P, S, PACK], BF16, align_bytes=64, name="x_bf")
        for j in range(PACK - 1):
            nc.vector.tensor_copy(x_bf[:, :, j], x_sb[j][:].indirect(offs_sb[:]))
        x_codes = sb.tile([P, S], U32, align_bytes=64, name="x_codes")
        x_scales = sb.tile([P, S], U8, align_bytes=64, name="x_scales")
        for cols in halves:
            nc.vector.tensor_copy(x_bf[:, cols, PACK - 1], x_sb[PACK - 1][:].indirect(entries(offs_sb, cols)))
            nc.vector.quantize_mx(out=x_codes[:, cols].bitcast(FP8X4), scales=x_scales[:, cols],
                                  in_=x_bf[:, cols].rearrange("p c j -> p (c j)"))

        w_bf = [sb.tile([P, 2, P, PACK], BF16, align_bytes=64, name=f"w_bf{u}") for u in range(2)]
        pairs = [slice(0, 4, 3), slice(1, 3)]

        def dealt(copy, h, u, first, last):
            copy(w_bf[u][:, :, first:last, 2 * h : 2 * h + 2].rearrange("p i (c e) j -> p c i e j", e=2),
                 w_sb[h][:].rearrange("p j (c e t) -> p c t e j", e=2, t=PACK)[:, first // 2 : last // 2, pairs[u]])

        for u in range(2):
            dealt(nc.scalar.copy, 0, u, 0, P)
        dealt(nc.vector.tensor_copy, 1, 0, 0, P)
        dealt(nc.vector.tensor_copy, 1, 1, SCALAR_GROUPS, P)
        dealt(nc.scalar.copy, 1, 1, 0, SCALAR_GROUPS)

        def quantised_w(u, first, last):
            count = last - first
            codes = sb.tile([P, count * P], U32, align_bytes=64, name=f"w_codes{u}_{first}")
            scales = sb.tile([P, count * P], U8, align_bytes=64, name=f"w_scales{u}_{first}")
            nc.vector.quantize_mx(out=codes[:].bitcast(FP8X4), scales=scales[:],
                                  in_=w_bf[u][:, first:last].rearrange("p i g j -> p (i g j)"))
            return [(codes[:, i * P : (i + 1) * P], scales[:, i * P : (i + 1) * P]) for i in range(count)]

        def product(out, w_plane, cols):
            codes, scales = w_plane
            nc.tensor.matmul_mx(out=out, lhsT=codes.bitcast(FP8X4), lhsT_scale=scales,
                                rhs=x_codes[:, cols].bitcast(FP8X4), rhs_scale=x_scales[:, cols], start=True, stop=True)

        (w_plane3,) = quantised_w(0, 1, 2)
        sums3_first = psum.tile([P, HALF], F32, name="sums3_first")
        product(sums3_first[:], w_plane3, halves[0])
        (w_plane0,) = quantised_w(0, 0, 1)
        sums0 = [psum.tile([P, HALF], F32, name=f"sums0_{h}") for h in range(2)]
        for h, cols in enumerate(halves):
            product(sums0[h][:], w_plane0, cols)
        w_plane1, w_plane2 = quantised_w(1, 0, 2)
        sums1 = psum.tile([P, S], F32, name="sums1")
        product(sums1[:], w_plane1, whole)
        sums2_first = psum.tile([P, HALF], F32, name="sums2_first")
        product(sums2_first[:], w_plane2, halves[0])
        sums23_second = psum.tile([P, 2, HALF], F32, name="sums23_second")
        product(sums23_second[:, 0, :], w_plane2, halves[1])
        product(sums23_second[:, 1, :], w_plane3, halves[1])

        g_sb = sb.tile([P, PACK, S], F32, name="g_sb")
        o_sb = sb.tile([P, PACK, S], F32, name="o_sb")
        o_bf = [sb.tile([P, HALF, PACK], BF16, align_bytes=64, name=f"o_bf{h}") for h in range(2)]
        o_codes = [sb.tile([P, HALF], U32, align_bytes=64, name=f"o_codes{h}") for h in range(2)]
        o_scales = sb.tile([P, S], U8, align_bytes=64, name="o_scales")

        def window(t, cols):
            return scale_sb[t][:].indirect(entries(task_sb, cols))

        def picked_by_scalar(t, cols):
            nc.scalar.activation(g_sb[:, t, cols], window(t, cols), COPY)

        def picked_by_vector(t, cols):
            nc.vector.tensor_copy(g_sb[:, t, cols], window(t, cols))

        def scaled(planes, cols, sums):
            nc.vector.tensor_tensor(o_sb[:, planes, cols], sums, g_sb[:, planes, cols], MULT)

        def stored(planes, cols):
            nc.sync.dma_start(out_rows[:, planes, cols], o_sb[:, planes, cols])

        picked_by_vector(0, halves[0])
        picked_by_scalar(0, halves[1])
        y3_first = sb.tile([P, HALF], F32, name="y3_first", tag="scale_sb0")
        nc.scalar.copy(y3_first[:], sums3_first[:])
        for h, cols in enumerate(halves):
            scaled(0, cols, sums0[h][:])
        stored(0, whole)

        picked_by_scalar(1, halves[0])
        picked_by_vector(1, halves[1])
        for cols in halves:
            scaled(1, cols, sums1[:, cols])
        stored(1, whole)

        last_pair = slice(2, 4)
        for cols in halves:
            picked_by_scalar(2, cols)
        scaled(2, halves[0], sums2_first[:])
        picked_by_scalar(3, halves[1])
        first_quarters = [slice(0, S // 4), slice(S // 4, HALF)]
        for cols in first_quarters:
            nc.vector.tensor_tensor(o_sb[:, 3, cols], window(3, cols), y3_first[:, cols], MULT)
        stored(last_pair, halves[0])
        quarters = [slice(HALF, HALF + S // 4), slice(HALF + S // 4, S)]
        for cols in quarters:
            scaled(last_pair, cols, sums23_second[:, :, cols.start - HALF : cols.stop - HALF])
        stored(last_pair, halves[1])

        def rounded(copy, h, cols):
            part = slice(cols.start - h * HALF, cols.stop - h * HALF)
            copy(o_bf[h][:, part, :].rearrange("p (c i) t -> p c t i", i=2),
                 o_sb[:, :, cols].rearrange("p t (c i) -> p c t i", i=2))

        for cols in first_quarters:
            rounded(nc.scalar.copy, 0, cols)
        rounded(nc.vector.tensor_copy, 1, quarters[0])
        rounded(nc.vector.tensor_copy, 1, slice(quarters[1].start, S - SCALAR_ROUNDS))
        rounded(nc.scalar.copy, 1, slice(S - SCALAR_ROUNDS, S))
        for h, cols in enumerate(halves):
            nc.vector.quantize_mx(out=o_codes[h][:].bitcast(FP8X4), scales=o_scales[:, cols],
                                  in_=o_bf[h][:].rearrange("p c t -> p (c t)"))
            nc.sync.dma_start(out_words[:, cols], o_codes[h][:].bitcast(I32))

        for q in range(4):
            queue = nc.scalar if q % 2 else nc.sync
            queue.dma_start(out_scales[4 * q : 4 * q + 4, :], o_scales[32 * q : 32 * q + 4, :].bitcast(I32))
